import numpy as np
CORES = [24,26,29,31,48,50,53,55]
N = 8
R, T, B, CAPP = 8192, 2048, 64, 512
LOW = np.float32(-201 * 2.0 ** 92)
def entries(a): return a.T.reshape(-1)
def pack(v, P): return np.ascontiguousarray(np.asarray(v, np.int32).reshape(-1, P).T)
def table(rng, how, c=()):
    t = rng.standard_normal((N, 128, R), dtype=np.float32); k = np.arange(128) if how == "neg" else rng.permutation(128)[:16]
    t[:, k] = -0.125 - np.abs(t[:, k])
    if len(c): t[(c // R)[:, None], rng.permutation(128)[:16][None, :], (c % R)[:, None]] = LOW
    return t
def lists(rng, how):
    O = np.stack([rng.permutation(np.repeat(np.arange(N), CAPP))[:T] for r in range(N)])
    if how in ("astride", "early"): P = rng.permutation(N)[:T // CAPP]; O = np.stack([rng.permutation(np.repeat(P, CAPP)) for r in range(N)])
    I = R * O + rng.integers(0, R, (N, T))
    if how == "late": u = rng.random((N, T)); I = np.where(u < 0.5, R * O + np.where(u < 0.25, 0, R - 1), I)
    s = np.concatenate([[0], rng.integers(1 - T // 2, T // 2 + 1, N - 1), [int(rng.integers(1 - T // 2, 1))]])
    if how == "astride":
        z = int(rng.integers(1, N - 1)); k = int(rng.integers(0, B - 1)); s[1:z] = -rng.integers(1, T, z - 1); s[z] = -T; s[z + 1] = T; s[z + 2:N] = rng.integers(1, T, N - z - 2); s[N] = 0
    if how == "early": s[1:] = -T
    if how == "late": s[1:N] = T; s[N] = 0
    if how == "void":
        w = int(rng.integers(3, N - 1)); z = int(rng.integers(1, w - 1)); s[z] = int(rng.integers(1, T // 2 + 1)); s[z + 1] = s[z] - T; s[w:] = s[w] - T * np.arange(N + 1 - w)
    S = T * np.arange(N + 1) + s
    E = np.concatenate([np.append(np.sort(rng.integers(S[q], S[q + 1] + 1, B - 1)), S[q + 1]) for q in range(N)])
    if how == "astride":
        E[B * z:B * z + B - 1] = np.concatenate([np.sort(rng.integers(S[z], T * z - T // 2 + 1, k)), np.sort(rng.integers(T * z + T + T // 2, S[z + 1], B - 2 - k)), [S[z + 1] - 1]])
        L = max(N * T - 1, S[N - 1]); E[N * B - B:N * B - 1] = np.minimum(E[N * B - B:N * B - 1], L); E[N * B - 2] = L
        E += np.isin(E, np.setdiff1d(T * np.arange(1, N), S[z:z + 2]))
    if how == "neg":
        K = rng.random(N * B) < 0.5; K[0] = False; K[B - 1::B] = True; j = np.flatnonzero(K); E = E[j[np.searchsorted(j, np.arange(N * B))]]
    if how == "void":
        k = np.sort(np.stack([B * q + 1 + rng.permutation(B - 2)[:3] for q in range(N)]), axis=1); v = E[k]; v[:, 2] = S[1:]
        E = np.concatenate([[0], v.reshape(-1)])[np.searchsorted(k.reshape(-1), np.arange(N * B), side="right")]
    d = {"idx": np.stack([pack(i, 16) for i in I]), "end": np.stack([pack(E, 16)] * N)}
    if how == "neg":
        n = np.diff(np.concatenate([[0], E])).reshape(N, B); b = B * np.arange(N) + ((n > 0) * (1 + rng.random((N, B)))).argmax(axis=1)
        d["tab"] = table(rng, "neg", I.reshape(-1)[np.isin(np.searchsorted(E, np.arange(N * T), side="right"), b)])
    return d
def setup_inputs(rng):
    return dict({"tab": table(rng, "uniform")}, **lists(rng, "uniform"))
def setup_inputs_astride(rng):
    d = setup_inputs(rng); d.update(lists(rng, "astride"))
    for k in ("tab",): d[k] = (d[k].astype(np.float32) * 1048576.0).astype(d[k].dtype)
    return d
def setup_inputs_early(rng):
    d = setup_inputs(rng); d.update(lists(rng, "early"))
    for k in ("tab",): d[k] = (d[k].astype(np.float32) * (1 / 1024.0)).astype(d[k].dtype)
    return d
def setup_inputs_late(rng):
    d = setup_inputs(rng); d.update(lists(rng, "late"))
    return d
def setup_inputs_neg(rng):
    d = setup_inputs(rng); d.update(lists(rng, "neg"))
    return d
def setup_inputs_void(rng):
    d = setup_inputs(rng); d.update(lists(rng, "void"))
    return d
def check_inputs(x):
    bad = []
    if x["idx"].min() < 0 or x["idx"].max() >= N * R: bad.append("idx out of range")
    if x["end"].min() < 0 or x["end"].max() >= N * T + 1: bad.append("end out of range")
    if (x["end"] != x["end"][:1]).any(): bad.append("end differs from rank to rank")
    v = entries(x["end"][0]).astype(np.int64); s = v[B - 1::B]
    if (np.diff(v) < 0).any(): bad.append("end falls")
    if any(s[q - 1] > T * (q + 1) or (s[q - 1] < T * (q - 1) and s[q - 1] != s[N - 1]) for q in range(1, N)): bad.append("an entry belongs to a bag of a rank that is more than one away from its holder")
    if max(int(np.bincount(entries(a) // R, minlength=N).max()) for a in x["idx"]) > CAPP: bad.append("more than CAPP entries of a rank's idx point into one rank's part of the table")
    t = x["tab"].astype(np.float32)
    if t.min() < np.float32(-1e30) or t.max() > np.float32(1e30): bad.append("tab beyond -1e30 to 1e30")
    return bad
def reference(tab, idx, end):
    A = np.concatenate(list(tab), axis=1)
    G = A[:, np.concatenate([entries(a) for a in idx])]
    Y = np.zeros((128, N * B), tab.dtype)
    for r in range(N):
        c = np.concatenate([[0], entries(end[r])])
        for b in range(B * r, B * r + B):
            if c[b + 1] > c[b]: Y[:, b] = G[:, c[b]:c[b + 1]].max(axis=1)
    return {"y": np.stack([Y[:, B * r:B * r + B] for r in range(N)])}

@@ -1,0 +1,475 @@
+from concourse.bass import DstId, RemoteDMATransfer
+from concourse.mybir import dt, AluOpType, AxisListType, ActivationFunctionType
+
+W = 80
+HB = 2048
+
+SCRATCH = {
+    "v": ("sbuf", [128, 128], "int32"), "endw": ("sbuf", [16, 32], "int32"), "erow": ("sbuf", [1, 192], "int32"),
+    "aa": ("sbuf", [128, 2048], "bfloat16"), "bb": ("sbuf", [128, 1024], "bfloat16"),
+    "win": ("sbuf", [128, 132], "float32"), "rx": ("sbuf", [128, 8 * W], "float16"),
+    "tw": ("sbuf", [128, 8196], "float32"), "cm": ("sbuf", [128, 128], "float32"),
+    "nl": ("sbuf", [128, 256], "float32"), "gl": ("sbuf", [128, 256], "float32"), "fl": ("sbuf", [128, 64], "float32"),
+}
+for _h in range(2):
+    for _n, _w, _d in (("mark", 2496, "bfloat16"), ("gd", HB, "float32"), ("run", HB + 4, "float32"), ("pick", 320, "float32")):
+        SCRATCH["%s%d" % (_n, _h)] = ("sbuf", [128, _w], _d)
+for _b in range(8):
+    SCRATCH["ps%d" % _b] = ("psum", [128, 512], "float32")
+LAY = {}
+for _a, _d, _l in (
+    ("ai", "int32", "pi 4 ri 4 ii 4 fr 144 frr 128 fri 128 part 128 h4i 128 oli 128 ohi 128 eri 192 eci 12 bq 32 b0i 20 b1i 20"),
+    ("ah", "float16", "bo 128 t1 128 nt 128 sel 16 selm 16 selr 16 seln 16 zz 144 ones 128 o4 128 ic 128 m4 128 h4 128 "
+                      "ol 128 oh 128 erh 192 mk 192 yy 192 s_o 128 s_a 128 s_d 128 s_b 128 base0 20 base1 20"),
+    ("af", "float32", "cf 8 rep 128 onef 128 big 4 l3 32 pay 64 endf 32 erf 192 trash 20 eb 80 ne 64 ze 64 zf 64 "
+                      "ya 64 yb 64 yc 64 yd 64 ye 64 nd0 20 nd1 20 pt0 20 pt1 20 sa0 20 sa1 20 sb0 20 sb1 20 pk0 20 pk1 20"),
+    ("ab", "bfloat16", "iob 128 ta 512 src 320"),
+    ("au", "uint16", "xo0 128 xo1 128 sc0 20 sc1 20 po0 20 po1 20 ecl 12"),
+):
+    _o = 0
+    _p = _l.split()
+    for _k in range(0, len(_p), 2):
+        LAY[_p[_k]] = (_a, _o, int(_p[_k + 1]))
+        _o += int(_p[_k + 1])
+    SCRATCH[_a] = ("sbuf", [128, _o], _d)
+
+_NAMES = ("ldi", "lde", "ldr", "ldt", "st", "nx", "fx", "ls", "ne2", "gx", "ff",
+          "io", "iom", "k_ri", "k_cf", "k_fr", "k_bo", "k_c", "bg0", "bg", "tws", "rus",
+          "endf", "eri", "erh", "p_e", "eci", "ecl", "p_eb", "mk", "part", "o4", "ic", "s4", "s4b", "win0", "win",
+          "m4", "h4i", "h4", "oli", "olh", "p_ol", "pay", "p_l3", "l3", "ta", "yy", "p_x", "pad", "tx",
+          "k_s", "k_d", "bq", "bi", "bs", "src0", "src", "erf", "p_z", "ebz", "eb", "ne", "ze", "zf", "mrk", "mrk2",
+          "cm", "ya", "yb", "yc", "yd", "ye")
+SEMAPHORES = list(_NAMES) + ["c%d" % i for i in range(16)]
+for _h in range(2):
+    SEMAPHORES += ["%s%d" % (n, _h) for n in ("p_xl", "p_p", "xo", "nd", "pt", "sa", "sb", "sc", "sct", "pk", "po",
+                                               "ga", "gb", "gc", "gd", "ra", "rb", "rc", "rd", "pik", "pib")]
+
+
+def routes(T, topo):
+    cores = list(T.cores)
+    chips = []
+    for c in cores:
+        if topo.chip(c) not in chips:
+            chips.append(topo.chip(c))
+    ranks = [[r for r in range(len(cores)) if topo.chip(cores[r]) == ch] for ch in chips]
+    gates = []
+    for h in range(2):
+        far = [cores[r] for r in ranks[1 - h]]
+        ok = [c for c in range(64) if topo.chip(c) == chips[h] and all(topo.may_write(c, f) for f in far)]
+        gates.append(ok[:len(far)])
+    return cores, chips, ranks, gates
+
+
+def split(mask, parts):
+    bits = [b for b in range(mask.bit_length()) if mask >> b & 1]
+    n = len(bits) // parts
+    return [sum(1 << b for b in bits[k * n:(k + 1) * n]) for k in range(parts)]
+
+
+def rank_program(g, core, T, topo):
+    cores, chips, ranks, gates = routes(T, topo)
+    q = T.rank_of(core)
+    if topo.chip(core) not in chips:
+        return
+    h = chips.index(topo.chip(core))
+    f = 1 - h
+    gate = core in gates[h]
+    if q is None and not gate:
+        return
+    near = ranks[h]
+    S = T.sem
+
+    def did(c):
+        a = topo.addr(c)
+        return DstId(rid=a[0], pnc=a[1])
+
+    farrank = ranks[f][gates[h].index(core)] if gate else None
+    farcore = cores[farrank] if gate else None
+    tiles = T.rx[:, near[0] * W:(near[0] + len(near)) * W]
+    if q is None:
+        g.wait_ge(S.nx, 16 * len(near))
+        a = topo.addr(farcore)
+        g.remote_dma(tiles, tiles, S.fx, S.ls, a[1], a[0], topo.mask(core, farcore))
+        g.wait_ge(S.gx, 4 * len(near))
+        g.remote_dma_fused([RemoteDMATransfer(srcs=[T.gl[:, k * 64:(k + 1) * 64] for k in range(len(near))], dsts=[T.fl[:]],
+                                              dst_ids=[did(farcore)], dma_engine_mask=topo.mask(core, farcore),
+                                              remote_sem=S.ff, alu_op=2)], local_sem=S.ls)
+        g.wait_ge(S.ls, 16)
+        return
+
+    A = AluOpType
+    F = ActivationFunctionType
+    v, s_, pe, sy = g.vector, g.scalar, g.tensor, g.sync
+    cnt = {}
+    seen = {}
+
+    def V(n, a=0, b=None, st=1, r=128):
+        ar, o, w = LAY[n]
+        b = w if b is None else b
+        return T[ar][0:r, o + a:o + b:st] if st > 1 else T[ar][0:r, o + a:o + b]
+
+    def inc(ins, name):
+        ins.then_inc(S[name], 1)
+        cnt[name] = cnt.get(name, 0) + 1
+
+    def wt(tag, eng, *names):
+        for n in names:
+            key = (tag, n)
+            if seen.get(key) != cnt[n]:
+                eng.wait_ge(S[n], cnt[n])
+                seen[key] = cnt[n]
+
+    def wv(*n):
+        wt("v", v, *n)
+
+    def wa(*n):
+        wt("a", s_, *n)
+
+    def wp(*n):
+        wt("p", pe, *n)
+
+    def c0(s):
+        return min(max(4 * (s - 1), 0), 20)
+
+    mm = pe.matmul
+    sy.dma_start(T.endw[:], T.end[:]).then_inc(S.lde, 16)
+    s_.dma_start(T.erow[:], T.end[:, c0(q):c0(q) + 12]).then_inc(S.ldr, 16)
+    for k in range(8):
+        (sy if k % 2 else s_).dma_start(T.v[16 * k:16 * k + 16, :], T.idx[:]).then_inc(S.ldi, 16)
+    for k in range(4):
+        sy.dma_start(T.tw[:, 4 + 2048 * k:4 + 2048 * (k + 1)], T.tab[:, 2048 * k:2048 * (k + 1)]).then_inc(S.ldt, 16)
+    cnt["lde"] = 16
+    cnt["ldr"] = 16
+    cnt["ldi"] = 128
+    cnt["ldt"] = 64
+    inc(g.iota(V("pi", 0, 1), [[1, 1]], 0, 1), "io")
+    inc(g.iota(V("fr"), [[1, 144]], 0, 0), "io")
+    inc(g.iota(V("trash"), [[16, 20]], HB + 1, 1, allow_small_or_imprecise_dtypes=True), "iom")
+    nmark = T["mark%d" % h]
+    fmark = T["mark%d" % f]
+    inc(g.iota(nmark[:, 0:HB], [[0, HB]], 1, 0, allow_small_or_imprecise_dtypes=True), "iom")
+    wv("io")
+    ri, ii = V("ri", 0, 1), V("ii", 0, 1)
+    fr = V("fr", 0, 128)
+    inc(v.tensor_scalar(ri, V("pi", 0, 1), 4, None, A.arith_shift_right), "k_ri")
+    inc(v.tensor_scalar(ii, V("pi", 0, 1), 15, None, A.bitwise_and), "k_ri")
+    inc(v.tensor_scalar(V("frr"), fr, 4, None, A.arith_shift_right), "k_fr")
+    inc(v.tensor_scalar(V("fri"), fr, 15, None, A.bitwise_and), "k_fr")
+    wv("k_ri")
+
+    def col(k, n=128):
+        return V("cf", k, k + 1, r=n)
+
+    inc(v.tensor_copy(col(0), ri), "k_cf")
+    inc(v.tensor_copy(col(1), ii), "k_cf")
+    inc(v.tensor_scalar(col(2), ri, 16.0, None, A.mult), "k_cf")
+    inc(v.tensor_scalar(col(3), ri, 16.0, 15.0, A.mult, A.add), "k_cf")
+    inc(v.tensor_scalar(col(4), ii, 1.0, None, A.add), "k_cf")
+    inc(v.tensor_scalar(col(5), ii, -15.0, None, A.add), "k_cf")
+    inc(v.tensor_scalar(col(6), ri, float(q), None, A.is_equal), "k_cf")
+    inc(v.tensor_scalar(col(7), ri, float(q), -1.0, A.is_equal, A.mult), "k_cf")
+    wv("k_cf", "k_fr")
+    inc(v.tensor_scalar(V("bo"), V("frr"), col(0), None, A.is_equal), "k_bo")
+    inc(v.tensor_scalar(V("t1"), V("fri"), col(1), -1.0, A.is_le, A.mult), "k_bo")
+    inc(v.tensor_scalar(V("ones"), fr, 0.0, None, A.is_ge), "k_c")
+    inc(v.tensor_scalar(V("rep", r=16), V("fri", r=16), col(1, 16), None, A.is_equal), "k_c")
+    inc(v.tensor_scalar(V("sel"), V("fr", 0, 16), col(1), None, A.is_equal), "k_c")
+    inc(v.tensor_scalar(V("selm"), V("fr", 0, 16), col(1), -16.0, A.is_equal, A.mult), "k_c")
+    inc(v.tensor_scalar(V("selr"), V("fr", 0, 16), col(1), col(2), A.is_equal, A.mult), "k_c")
+    inc(v.tensor_scalar(V("seln"), V("fr", 0, 16), col(1), -1.0, A.is_equal, A.mult), "k_c")
+    wv("k_bo")
+    inc(v.tensor_tensor(V("nt"), V("bo"), V("t1"), A.mult), "k_c")
+    inc(v.tensor_scalar(V("zz"), V("fr"), col(3), None, A.is_equal), "k_c")
+    inc(v.tensor_copy(V("iob"), fr), "k_c")
+    inc(v.memset(V("big"), 2.0 ** 99), "bg0")
+    inc(v.memset(T.win[:, 0:1], 0.0), "win0")
+    inc(v.memset(T.win[:, 129:130], 0.0), "win0")
+    wv("bg0")
+    inc(v.tensor_scalar(T.tw[:, 0:4], V("big"), -2.0, None, A.mult), "tws")
+    for k in range(2):
+        inc(v.tensor_scalar(T["run%d" % k][:, 0:4], V("big"), -2.0, None, A.mult), "rus")
+    inc(v.tensor_copy(T.rx[:, q * W + 76:q * W + 80], V("fr", 0, 4)), "pad")
+    wv("lde")
+    inc(v.tensor_copy(V("endf", r=16), T.endw[:]), "endf")
+    wv("ldr")
+    inc(v.tensor_scalar(V("eri", r=1), T.erow[:], 15, None, A.bitwise_and), "eri")
+    wp("k_c", "endf")
+    inc(mm(T.ps5[:, 0:32], V("rep", r=16), V("endf", r=16), True, True), "p_e")
+    wv("ldi")
+    inc(v.tensor_scalar(V("part"), T.v[:], 13, None, A.arith_shift_right), "part")
+    wv("eri")
+    inc(v.tensor_copy(V("erh", r=1), V("eri", r=1)), "erh")
+    wv("part", "k_c")
+    inc(v.tensor_scalar(V("o4"), V("part"), col(0), None, A.is_equal), "o4")
+    inc(v.tensor_scalar(V("oli", r=16), T.v[0:16, :], 127, None, A.bitwise_and), "oli")
+    wv("o4")
+    inc(v.tensor_tensor_scan(V("ic"), V("ones"), V("o4"), 0.0, A.mult, A.add), "ic")
+    inc(v.tensor_scalar(V("ohi", r=16), T.v[0:16, :], 8064, None, A.bitwise_and), "oli")
+    wp("o4", "k_bo")
+    mm(T.ps0[:, 0:128], V("nt"), V("o4"), True, False)
+    wp("ic")
+    inc(mm(T.ps0[:, 0:128], V("bo"), V("ic"), False, True), "s4")
+    mm(T.ps3[:, 0:128], V("nt"), V("o4"), True, False)
+    inc(mm(T.ps3[:, 0:128], V("bo"), V("ic"), False, True), "s4b")
+    wv("oli")
+    inc(v.tensor_scalar(V("ol", r=16), V("oli", r=16), 4.0, None, A.add), "olh")
+    inc(v.tensor_copy(V("oh", r=16), V("ohi", r=16)), "olh")
+    wp("olh")
+    mm(T.ps7[:, 0:16], V("ol", r=16), V("sel", r=16), True, True)
+    mm(T.ps7[:, 16:32], V("oh", r=16), V("sel", r=16), True, True)
+    mm(T.ps7[:, 32:48], V("ol", r=16), V("seln", r=16), True, True)
+    inc(mm(T.ps7[:, 48:64], V("oh", r=16), V("seln", r=16), True, True), "p_ol")
+    wp("erh")
+    for k in range(12):
+        x = mm(T.ps6[:, 16 * k:16 * k + 16], V("ones", r=1), V("erh", k, 192, 12, 1), True, True)
+    inc(x, "p_eb")
+    wv("s4")
+    inc(v.tensor_scalar(V("h4i"), T.ps0[:, 0:128], -7.5, 1.0 / 16, A.add, A.mult), "h4i")
+    inc(v.tensor_tensor(V("m4"), T.ps0[:, 0:128], V("o4"), A.mult), "m4")
+    wv("h4i")
+    inc(v.tensor_tensor(V("h4"), V("h4i"), V("o4"), A.mult), "h4")
+    wa("s4b", "win0")
+    inc(s_.activation(T.win[:, 1:129], T.ps3[:, 0:128], F.Identity), "win")
+    wp("m4", "h4")
+    mm(T.ps1[:, 0:16], V("m4"), V("sel"), True, False)
+    mm(T.ps1[:, 0:16], V("o4"), V("selr"), False, False)
+    mm(T.ps1[:, 0:16], V("h4"), V("selm"), False, True)
+    inc(mm(T.ps1[:, 16:32], V("h4"), V("sel"), True, True), "p_l3")
+    wv("p_e")
+    inc(v.tensor_scalar(V("eci"), T.ps5[:, c0(q):c0(q) + 12], 8.5 - 2048.0 * q, 1.0 / 16, A.add, A.mult), "eci")
+    wv("p_ol")
+    inc(v.tensor_copy(V("pay"), T.ps7[:, 0:64]), "pay")
+    wv("eci")
+    inc(v.tensor_scalar(V("ecl"), V("eci"), 0.0, 129.0, A.max, A.min), "ecl")
+    wv("p_l3")
+    inc(v.tensor_copy(V("l3"), T.ps1[:, 0:32]), "l3")
+    wv("p_eb")
+    inc(v.tensor_scalar(V("mk"), T.ps6[:, 0:192], col(1), None, A.is_equal), "mk")
+    wv("ecl", "win", "mk", "win0")
+    inc(v.tensor_tensor(V("yy"), T.win[:, 0:130].indirect(V("ecl")), V("mk"), A.mult), "yy")
+    ev, od = list(range(0, 16, 2)), list(range(1, 16, 2))
+    wa("l3", "pay", "k_c")
+    for i in od:
+        inc(s_.activation(V("ta", 32 * i, 32 * i + 32), V("iob", 0, 32), F.Abs, bias=V("l3", 16 + i, 17 + i), scale=-1.0), "ta")
+    wa("ta")
+    for i in od:
+        for d in range(2):
+            inc(s_.activation(T.bb[:, 64 * i + 32 * d:64 * i + 32 * d + 32], V("ta", 32 * i, 32 * i + 32), F.Relu,
+                              bias=V("pay", 16 * d + i, 16 * d + i + 1), scale=V("pay", 32 + 16 * d + i, 33 + 16 * d + i)), "c%d" % i)
+    wv("l3", "pay", "k_c")
+    for i in ev + od:
+        inc(v.tensor_scalar(T.aa[:, 128 * i:128 * i + 128], V("iob"), V("l3", i, i + 1), None, A.is_equal), "c%d" % i)
+        if i in ev:
+            for d in range(2):
+                inc(v.tensor_scalar(T.bb[:, 64 * i + 32 * d:64 * i + 32 * d + 32], V("iob", 0, 32), V("l3", 16 + i, 17 + i),
+                                    V("pay", 16 * d + i, 16 * d + i + 1), A.is_equal, A.mult), "c%d" % i)
+    wp("yy")
+    for b in range(16):
+        mm(T.ps2[:, 64:76], V("zz", 15 - b, 143 - b), V("yy", b, 192, 16), b == 0, b == 15)
+    order = ev + od
+    for i in order:
+        wp("c%d" % i)
+        x = mm(T.ps2[:, 0:64], T.aa[:, 128 * i:128 * i + 128], T.bb[:, 64 * i:64 * i + 64], i == order[0], i == order[-1])
+    inc(x, "p_x")
+    wv("p_x")
+    inc(v.tensor_copy(T.rx[:, q * W:q * W + 76], T.ps2[:, 0:76]), "tx")
+    own = T.rx[:, q * W:(q + 1) * W]
+    others = [cores[r] for r in near if r != q]
+    to = others + [c for c in gates[h] if T.rank_of(c) is None]
+    wt("g", g, "tx", "pad")
+    g.remote_dma_fused([RemoteDMATransfer(srcs=[own], dsts=[own] * len(to), dst_ids=[did(c) for c in to],
+                                          dma_engine_mask=topo.mask(core, to[0]), remote_sem=S.nx)], local_sem=S.ls)
+    nls = 16
+    cnt["nx"] = 16 * (len(near) - 1)
+    cnt["fx"] = 8
+    if gate:
+        wt("g", g, "nx")
+        a = topo.addr(farcore)
+        g.remote_dma(tiles, tiles, S.fx, S.ls, a[1], a[0], topo.mask(core, farcore))
+        nls += 8
+    inc(v.tensor_scalar(V("big", 1, 2), V("big", 0, 1), 4.0, None, A.mult), "bg")
+    inc(v.tensor_scalar(V("s_o"), V("fri"), col(1), col(6), A.is_equal, A.mult), "k_s")
+    inc(v.tensor_scalar(V("s_a"), V("fri"), col(4), col(6), A.is_equal, A.mult), "k_s")
+    inc(v.tensor_scalar(V("s_b"), V("fri"), col(5), col(7), A.is_equal, A.mult), "k_d")
+    inc(v.tensor_scalar(V("bq"), T.ps5[:, 0:32], -1023.5, 1.0 / 2048, A.add, A.mult), "bq")
+    inc(v.memset(V("src"), -2.0 ** 99), "src0")
+    wv("k_s")
+    inc(v.tensor_tensor(V("s_d"), V("s_o"), V("s_a"), A.subtract), "k_d")
+    wv("bq")
+    inc(v.tensor_scalar(V("b0i"), V("bq", 0, 20), 0.0, 4.0, A.max, A.min), "bi")
+    inc(v.tensor_scalar(V("b1i"), V("bq", 12, 32), -4.0, 0.0, A.add, A.max), "bi")
+    wv("src0")
+    inc(v.tensor_scalar(V("src"), V("src"), 2.0, None, A.mult), "src")
+    wv("bi")
+    inc(v.tensor_scalar(V("base0"), V("b0i"), 512.0, None, A.mult), "bs")
+    inc(v.tensor_scalar(V("base1"), V("b1i"), 4.0, 512.0, A.min, A.mult), "bs")
+    wa("bg", "iom")
+    inc(s_.activation(fmark[:, 0:HB], nmark[:, 0:HB], F.Copy, scale=V("big", 1, 2)), "mrk")
+    wa("mrk")
+    inc(s_.activation(nmark[:, 0:HB], nmark[:, 0:HB], F.Copy, scale=V("big", 1, 2)), "mrk2")
+
+    psx = {h: T.ps0, f: T.ps1}
+    psp = {h: T.ps3, f: T.ps4}
+    psd = {h: T.ps5, f: T.ps6}
+
+    def N(n, k):
+        return "%s%d" % (n, k)
+
+    def pe_half(k, arrived):
+        ps = psx[k]
+        bs = N("base", k)
+        P, D = psp[k], psd[k]
+        wp("k_s", "k_d", "bs")
+        mm(P[:, 0:20], V("s_o"), V(bs), True, False)
+        mm(D[:, 0:20], V("s_d"), V(bs), True, False)
+        mm(D[:, 1:20], V("s_b"), V(bs, 0, 19), False, False)
+        wp(arrived)
+        if k == h:
+            wp("tx")
+        for j, s in enumerate(ranks[k]):
+            mm(ps[:, 32 * j:32 * j + 32], V("s_o"), T.rx[:, s * W:s * W + 32], True, False)
+            x = mm(ps[:, 32 * j:32 * j + 32], V("s_o"), T.rx[:, s * W + 32:s * W + 64], False, True)
+        inc(x, N("p_xl", k))
+        last = ranks[k][-1]
+        for s in ranks[k]:
+            o = c0(s) - 12 * k
+            t = T.rx[:, s * W + 64:s * W + 76]
+            w = min(12, 19 - o)
+            x1 = mm(P[:, o:o + 12], V("s_o"), t, False, s == last)
+            mm(D[:, o:o + 12], V("s_d"), t, False, False)
+            x2 = mm(D[:, o + 1:o + 1 + w], V("s_b"), T.rx[:, s * W + 64:s * W + 64 + w], False, s == last)
+        inc(x1, N("p_p", k))
+        inc(x2, N("p_p", k))
+
+    def gathers(k):
+        for j in range(4):
+            wa(N("xo", k), "ldt", "tws")
+            inc(s_.activation(T[N("gd", k)][:, 512 * j:512 * j + 512],
+                              T.tw[:].indirect(V(N("xo", k), 32 * j, 32 * j + 32)), F.Copy), N("g" + "abcd"[j], k))
+
+    def lists(k):
+        def n(x):
+            return V(N(x, k))
+        wv(N("p_xl", k))
+        inc(v.tensor_copy(n("xo"), psx[k][:, 0:128]), N("xo", k))
+        wv(N("p_p", k), "iom")
+        inc(v.tensor_scalar(n("nd"), psd[k][:, 0:20], 0.0, None, A.is_gt), N("nd", k))
+        inc(v.tensor_tensor(n("pt"), psp[k][:, 0:20], V("trash"), A.subtract), N("pt", k))
+        wv(N("nd", k), N("pt", k))
+        inc(v.tensor_tensor(n("sa"), n("nd"), n("pt"), A.mult), N("sa", k))
+        inc(v.tensor_tensor(n("pk"), psp[k][:, 0:20], n("nd"), A.mult), N("pk", k))
+        wv(N("sa", k))
+        inc(v.tensor_tensor(n("sb"), n("sa"), V("trash"), A.add), N("sb", k))
+        wv(N("pk", k))
+        inc(v.tensor_copy(n("po"), n("pk")), N("po", k))
+        wv(N("sb", k))
+        inc(v.tensor_copy(n("sc"), n("sb")), N("sc", k))
+        wv(N("sc", k), "src", "mrk", "mrk2")
+        inc(v.tensor_copy(T[N("mark", k)][:].indirect(n("sc")), V("src")), N("sct", k))
+
+    def scans(k):
+        run = T[N("run", k)]
+        wv(N("sct", k), "rus")
+        for j in range(4):
+            wv(N("g" + "abcd"[j], k))
+            if j:
+                wv(N("r" + "abcd"[j - 1], k))
+            inc(v.tensor_tensor_scan(run[:, 4 + 512 * j:516 + 512 * j], T[N("mark", k)][:, 512 * j:512 * j + 512],
+                                     T[N("gd", k)][:, 512 * j:512 * j + 512], run[:, 3 + 512 * j:4 + 512 * j], A.min, A.max),
+                N("r" + "abcd"[j], k))
+
+    def picks(k):
+        e = 12 if k == 0 else 0
+        o = 0 if k == 0 else 8
+        names = [N("r" + c, k) for c in "abcd"]
+        wa(N("po", k), "rus", *names)
+        inc(s_.activation(T[N("pick", k)][:, 16 * o:16 * o + 192],
+                          T[N("run", k)][:, 3:HB + 4].indirect(V(N("po", k), o, o + 12)), F.Copy), N("pik", k))
+        wv(N("po", k), *names)
+        inc(v.tensor_copy(T[N("pick", k)][:, 16 * e:16 * e + 128],
+                          T[N("run", k)][:, 3:HB + 4].indirect(V(N("po", k), e, e + 8))), N("pib", k))
+
+    def piece(d):
+        if d in (3, 4):
+            return T.cm[:, 64 * (d - 3):64 * (d - 2)]
+        return T.pick0[:, 64 * d:64 * d + 64] if d < 3 else T.pick1[:, 64 * (d - 3):64 * (d - 2)]
+
+    pe_half(h, "nx")
+    lists(h)
+    gathers(h)
+    inc(v.tensor_copy(V("erf", r=1), T.erow[:]), "erf")
+    inc(v.memset(V("onef", r=1), 1.0), "erf")
+    lo = 4 * q - 1 - c0(q)
+    wp("erf")
+    for k in range(5):
+        if lo + k >= 0:
+            x = mm(T.ps7[:, 16 * k:16 * k + 16], V("onef", r=1), V("erf", lo + k, 192, 12, 1), True, True)
+    inc(x, "p_z")
+    scans(h)
+    picks(h)
+    done = [d for d in near if d not in (3, 4)]
+    rest = [d for d in near if d in (3, 4)][0]
+    send = [d for d in done if d != q]
+    full = topo.mask(core, others[0])
+    mine = T.nl[:, 64 * near.index(q):64 * near.index(q) + 64]
+    wt("g", g, N("pik", h))
+    ms = split(full, 4)
+    g.remote_dma_fused([RemoteDMATransfer(srcs=[piece(d)], dsts=[mine], dst_ids=[did(cores[d])], dma_engine_mask=ms[k],
+                                          remote_sem=S.ne2) for k, d in enumerate(send)], local_sem=S.ls)
+    nls += 4 * len(send)
+    b0 = 0
+    if lo < 0:
+        inc(v.memset(V("eb", 0, 16), 0.0), "ebz")
+        wv("ebz")
+        b0 = 16
+    wv("p_z")
+    inc(v.tensor_copy(V("eb", b0, 80), T.ps7[:, b0:80]), "eb")
+    wv("eb")
+    inc(v.tensor_tensor(V("ne"), V("eb", 16, 80), V("eb", 15, 79), A.is_gt), "ne")
+    wv("ne")
+    inc(v.tensor_scalar(V("ze"), V("ne"), -2.0 ** 99, 0.0, A.mult, A.add), "ze")
+    wv("ze")
+    inc(v.tensor_scalar(V("zf"), V("ze"), 2.0, None, A.mult), "zf")
+    pe_half(f, "fx")
+    lists(f)
+    gathers(f)
+    scans(f)
+    picks(f)
+    wv("pib0", "pib1")
+    inc(v.tensor_tensor(T.cm[:], T.pick0[:, 192:320], T.pick1[:, 0:128], A.max), "cm")
+    wt("g", g, "cm", N("pik", f))
+    tr = []
+    for k, c in enumerate(gates[h]):
+        if c != core:
+            tr.append(RemoteDMATransfer(srcs=[piece(ranks[f][k])], dsts=[T.gl[:, 64 * near.index(q):64 * near.index(q) + 64]],
+                                        dst_ids=[did(c)], dma_engine_mask=ms[k], remote_sem=S.gx))
+    g.remote_dma_fused(tr, local_sem=S.ls)
+    nls += 4 * len(tr)
+    if rest != q:
+        a = topo.addr(cores[rest])
+        g.remote_dma(mine, piece(rest), S.ne2, S.ls, a[1], a[0], full)
+        nls += 16
+    if gate:
+        g.wait_ge(S.gx, 4 * (len(near) - 1))
+        g.remote_dma_fused([RemoteDMATransfer(srcs=[piece(farrank) if r == q else T.gl[:, 64 * k:64 * k + 64] for k, r in enumerate(near)],
+                                              dsts=[T.fl[:]], dst_ids=[did(farcore)], dma_engine_mask=topo.mask(core, farcore),
+                                              remote_sem=S.ff, alu_op=2)], local_sem=S.ls)
+        nls += 8
+    cnt["ne2"] = (4 if q in done else 16) * (len(near) - 1)
+    cnt["ff"] = 8
+    wv("cm", N("pik", h), "zf")
+    inc(v.tensor_tensor(V("ya"), piece(q), V("zf"), A.max), "ya")
+    last = "ya"
+    wv("ne2")
+    names = ["yb", "yc", "yd"]
+    for k, r in enumerate([r for r in near if r != q]):
+        wv(last)
+        j = near.index(r)
+        inc(v.tensor_tensor(V(names[k]), V(last), T.nl[:, 64 * j:64 * j + 64], A.max), names[k])
+        last = names[k]
+    wv(last, "ff")
+    inc(v.tensor_tensor(V("ye"), V(last), T.fl[:], A.max), "ye")
+    wt("sy", sy, "ye")
+    sy.dma_start(T.y[:], V("ye")).then_inc(S.st, 16)
+    sy.wait_ge(S.st, 16)
+    g.wait_ge(S.ls, nls)

@@ -3,12 +3,12 @@ from concourse.mybir import dt, AluOpType, AxisListType, ActivationFunctionType
 
 W = 80
 HB = 2048
+CUT = (0, 7168, 8192)
 
 SCRATCH = {
     "v": ("sbuf", [128, 128], "int32"), "endw": ("sbuf", [16, 32], "int32"), "erow": ("sbuf", [1, 192], "int32"),
-    "aa": ("sbuf", [128, 2048], "bfloat16"), "bb": ("sbuf", [128, 1024], "bfloat16"),
-    "win": ("sbuf", [128, 132], "float32"), "rx": ("sbuf", [128, 8 * W], "float16"),
-    "tw": ("sbuf", [128, 8196], "float32"), "cm": ("sbuf", [128, 128], "float32"),
+    "aa": ("sbuf", [128, 2048], "bfloat16"), "bb": ("sbuf", [128, 1024], "bfloat16"), "win": ("sbuf", [128, 132], "float32"),
+    "rx": ("sbuf", [128, 8 * W], "float16"), "tw": ("sbuf", [128, 8196], "float32"),
     "nl": ("sbuf", [128, 256], "float32"), "gl": ("sbuf", [128, 256], "float32"), "fl": ("sbuf", [128, 64], "float32"),
 }
 for _h in range(2):
@@ -21,9 +21,9 @@ for _a, _d, _l in (
     ("ai", "int32", "pi 4 ri 4 ii 4 fr 144 frr 128 fri 128 part 128 h4i 128 oli 128 ohi 128 eri 192 eci 12 bq 32 b0i 20 b1i 20"),
     ("ah", "float16", "bo 128 t1 128 nt 128 sel 16 selm 16 selr 16 seln 16 zz 144 ones 128 o4 128 ic 128 m4 128 h4 128 "
                       "ol 128 oh 128 erh 192 mk 192 yy 192 s_o 128 s_a 128 s_d 128 s_b 128 base0 20 base1 20"),
-    ("af", "float32", "cf 8 rep 128 onef 128 big 4 l3 32 pay 64 endf 32 erf 192 trash 20 eb 80 ne 64 ze 64 zf 64 "
+    ("af", "float32", "cf 8 rep 128 onef 128 big 4 bgc 4 l3 32 pay 64 endf 32 erf 192 trash 20 eb 80 ne 64 ze 64 zf 64 "
                       "ya 64 yb 64 yc 64 yd 64 ye 64 nd0 20 nd1 20 pt0 20 pt1 20 sa0 20 sa1 20 sb0 20 sb1 20 pk0 20 pk1 20"),
-    ("ab", "bfloat16", "iob 128 ta 512 src 320"),
+    ("ab", "bfloat16", "iob 128 ta 512 src 320 one 512"),
     ("au", "uint16", "xo0 128 xo1 128 sc0 20 sc1 20 po0 20 po1 20 ecl 12"),
 ):
     _o = 0
@@ -33,31 +33,15 @@ for _a, _d, _l in (
         _o += int(_p[_k + 1])
     SCRATCH[_a] = ("sbuf", [128, _o], _d)
 
-_NAMES = ("ldi", "lde", "ldr", "ldt", "st", "nx", "fx", "ls", "ne2", "gx", "ff",
-          "io", "iom", "k_ri", "k_cf", "k_fr", "k_bo", "k_c", "bg0", "bg", "tws", "rus",
-          "endf", "eri", "erh", "p_e", "eci", "ecl", "p_eb", "mk", "part", "o4", "ic", "s4", "s4b", "win0", "win",
-          "m4", "h4i", "h4", "oli", "olh", "p_ol", "pay", "p_l3", "l3", "ta", "yy", "p_x", "pad", "tx",
-          "k_s", "k_d", "bq", "bi", "bs", "src0", "src", "erf", "p_z", "ebz", "eb", "ne", "ze", "zf", "mrk", "mrk2",
-          "cm", "ya", "yb", "yc", "yd", "ye")
-SEMAPHORES = list(_NAMES) + ["c%d" % i for i in range(16)]
+SEMAPHORES = ["ldi", "lde", "ldr", "ldt", "st", "nx", "fx", "ls", "ne2", "gx", "ff", "go",
+              "io", "io1", "iom", "k_ri", "k_cf", "k_cg", "k_fr", "k_bo", "k_c", "k_z", "k_i", "bg0", "bg", "tws", "rus",
+              "endf", "eri", "erh", "p_e", "eci", "ecl", "p_eb", "mk", "part", "o4", "ic", "s4", "s4b", "win0", "win",
+              "m4", "h4i", "h4", "oli", "olh", "p_ol", "pay", "p_l3", "l3", "ta", "yy", "p_pp", "p_x", "pad", "ptx", "tx",
+              "k_s", "k_d", "bq", "bi", "bs", "src0", "src", "erf", "p_z", "ebz", "eb", "ne", "ze", "zf", "mrk0", "mrk1",
+              "cmf", "cmn", "ya", "yb", "yc", "yd", "ye"] + ["c%d" % i for i in range(16)]
 for _h in range(2):
     SEMAPHORES += ["%s%d" % (n, _h) for n in ("p_xl", "p_p", "xo", "nd", "pt", "sa", "sb", "sc", "sct", "pk", "po",
                                                "ga", "gb", "gc", "gd", "ra", "rb", "rc", "rd", "pik", "pib")]
-
-
-def routes(T, topo):
-    cores = list(T.cores)
-    chips = []
-    for c in cores:
-        if topo.chip(c) not in chips:
-            chips.append(topo.chip(c))
-    ranks = [[r for r in range(len(cores)) if topo.chip(cores[r]) == ch] for ch in chips]
-    gates = []
-    for h in range(2):
-        far = [cores[r] for r in ranks[1 - h]]
-        ok = [c for c in range(64) if topo.chip(c) == chips[h] and all(topo.may_write(c, f) for f in far)]
-        gates.append(ok[:len(far)])
-    return cores, chips, ranks, gates
 
 
 def split(mask, parts):
@@ -67,36 +51,48 @@ def split(mask, parts):
 
 
 def rank_program(g, core, T, topo):
-    cores, chips, ranks, gates = routes(T, topo)
     q = T.rank_of(core)
+    cores = list(T.cores)
+    chips = []
+    for c in cores:
+        if topo.chip(c) not in chips:
+            chips.append(topo.chip(c))
     if topo.chip(core) not in chips:
         return
+    ranks = [[r for r in range(len(cores)) if topo.chip(cores[r]) == ch] for ch in chips]
     h = chips.index(topo.chip(core))
     f = 1 - h
-    gate = core in gates[h]
+    near, far = ranks[h], ranks[f]
+    gates = [c for c in range(64) if topo.chip(c) == chips[h] and all(topo.may_write(c, cores[d]) for d in far)][:len(far)]
+    gate = core in gates
     if q is None and not gate:
         return
-    near = ranks[h]
     S = T.sem
+    fd = far[gates.index(core)] if gate else None
+    n3 = len(near) - (0 if q is None else 1)
 
     def did(c):
         a = topo.addr(c)
         return DstId(rid=a[0], pnc=a[1])
 
-    farrank = ranks[f][gates[h].index(core)] if gate else None
-    farcore = cores[farrank] if gate else None
-    tiles = T.rx[:, near[0] * W:(near[0] + len(near)) * W]
+    def pass_on():
+        t = T.rx[:, near[0] * W:(near[-1] + 1) * W]
+        a = topo.addr(cores[fd])
+        g.remote_dma(t, t, S.fx, S.ls, a[1], a[0], topo.mask(core, cores[fd]))
+
+    def fold(srcs):
+        g.remote_dma_fused([RemoteDMATransfer(srcs=srcs, dsts=[T.fl[:]], dst_ids=[did(cores[fd])], alu_op=2,
+                                              dma_engine_mask=topo.mask(core, cores[fd]), remote_sem=S.ff)], local_sem=S.ls)
+
     if q is None:
-        g.wait_ge(S.nx, 16 * len(near))
-        a = topo.addr(farcore)
-        g.remote_dma(tiles, tiles, S.fx, S.ls, a[1], a[0], topo.mask(core, farcore))
-        g.wait_ge(S.gx, 4 * len(near))
-        g.remote_dma_fused([RemoteDMATransfer(srcs=[T.gl[:, k * 64:(k + 1) * 64] for k in range(len(near))], dsts=[T.fl[:]],
-                                              dst_ids=[did(farcore)], dma_engine_mask=topo.mask(core, farcore),
-                                              remote_sem=S.ff, alu_op=2)], local_sem=S.ls)
+        g.wait_ge(S.nx, 16 * n3)
+        pass_on()
+        g.wait_ge(S.gx, 4 * n3)
+        fold([T.gl[:, 64 * k:64 * k + 64] for k in range(len(near))])
         g.wait_ge(S.ls, 16)
         return
 
+    me = near.index(q)
     A = AluOpType
     F = ActivationFunctionType
     v, s_, pe, sy = g.vector, g.scalar, g.tensor, g.sync
@@ -131,30 +127,36 @@ def rank_program(g, core, T, topo):
     def c0(s):
         return min(max(4 * (s - 1), 0), 20)
 
+    def N(n, k):
+        return "%s%d" % (n, k)
+
     mm = pe.matmul
+    ts, tt = v.tensor_scalar, v.tensor_tensor
     sy.dma_start(T.endw[:], T.end[:]).then_inc(S.lde, 16)
     s_.dma_start(T.erow[:], T.end[:, c0(q):c0(q) + 12]).then_inc(S.ldr, 16)
     for k in range(8):
         (sy if k % 2 else s_).dma_start(T.v[16 * k:16 * k + 16, :], T.idx[:]).then_inc(S.ldi, 16)
-    for k in range(4):
-        sy.dma_start(T.tw[:, 4 + 2048 * k:4 + 2048 * (k + 1)], T.tab[:, 2048 * k:2048 * (k + 1)]).then_inc(S.ldt, 16)
-    cnt["lde"] = 16
-    cnt["ldr"] = 16
-    cnt["ldi"] = 128
-    cnt["ldt"] = 64
+
+    def load(k):
+        sy.dma_start(T.tw[:, 4 + CUT[k]:4 + CUT[k + 1]], T.tab[:, CUT[k]:CUT[k + 1]]).then_inc(S.ldt, 16)
+
+    load(0)
+    cnt.update({"lde": 16, "ldr": 16, "ldi": 128, "ldt": 32, "nx": 16 * n3, "fx": 8, "ff": 8, "ne2": 4 * n3, "go": 1})
     inc(g.iota(V("pi", 0, 1), [[1, 1]], 0, 1), "io")
     inc(g.iota(V("fr"), [[1, 144]], 0, 0), "io")
+    inc(g.iota(V("one"), [[0, 512]], 1, 0, allow_small_or_imprecise_dtypes=True), "io1")
     inc(g.iota(V("trash"), [[16, 20]], HB + 1, 1, allow_small_or_imprecise_dtypes=True), "iom")
-    nmark = T["mark%d" % h]
-    fmark = T["mark%d" % f]
-    inc(g.iota(nmark[:, 0:HB], [[0, HB]], 1, 0, allow_small_or_imprecise_dtypes=True), "iom")
+    inc(v.memset(V("big"), 2.0 ** 99), "bg0")
+    inc(v.memset(T.win[:, 0:1], 0.0), "win0")
+    inc(v.memset(T.win[:, 129:130], 0.0), "win0")
+    wv("bg0")
+    inc(ts(V("bgc"), V("big"), 4.0, None, A.mult), "bg")
     wv("io")
-    ri, ii = V("ri", 0, 1), V("ii", 0, 1)
-    fr = V("fr", 0, 128)
-    inc(v.tensor_scalar(ri, V("pi", 0, 1), 4, None, A.arith_shift_right), "k_ri")
-    inc(v.tensor_scalar(ii, V("pi", 0, 1), 15, None, A.bitwise_and), "k_ri")
-    inc(v.tensor_scalar(V("frr"), fr, 4, None, A.arith_shift_right), "k_fr")
-    inc(v.tensor_scalar(V("fri"), fr, 15, None, A.bitwise_and), "k_fr")
+    ri, ii, fr = V("ri", 0, 1), V("ii", 0, 1), V("fr", 0, 128)
+    inc(ts(ri, V("pi", 0, 1), 4, None, A.arith_shift_right), "k_ri")
+    inc(ts(ii, V("pi", 0, 1), 15, None, A.bitwise_and), "k_ri")
+    inc(ts(V("frr"), fr, 4, None, A.arith_shift_right), "k_fr")
+    inc(ts(V("fri"), fr, 15, None, A.bitwise_and), "k_fr")
     wv("k_ri")
 
     def col(k, n=128):
@@ -162,49 +164,46 @@ def rank_program(g, core, T, topo):
 
     inc(v.tensor_copy(col(0), ri), "k_cf")
     inc(v.tensor_copy(col(1), ii), "k_cf")
-    inc(v.tensor_scalar(col(2), ri, 16.0, None, A.mult), "k_cf")
-    inc(v.tensor_scalar(col(3), ri, 16.0, 15.0, A.mult, A.add), "k_cf")
-    inc(v.tensor_scalar(col(4), ii, 1.0, None, A.add), "k_cf")
-    inc(v.tensor_scalar(col(5), ii, -15.0, None, A.add), "k_cf")
-    inc(v.tensor_scalar(col(6), ri, float(q), None, A.is_equal), "k_cf")
-    inc(v.tensor_scalar(col(7), ri, float(q), -1.0, A.is_equal, A.mult), "k_cf")
+    inc(ts(col(2), ri, 16.0, None, A.mult), "k_cf")
+    inc(ts(col(3), ri, 16.0, 15.0, A.mult, A.add), "k_cf")
     wv("k_cf", "k_fr")
-    inc(v.tensor_scalar(V("bo"), V("frr"), col(0), None, A.is_equal), "k_bo")
-    inc(v.tensor_scalar(V("t1"), V("fri"), col(1), -1.0, A.is_le, A.mult), "k_bo")
-    inc(v.tensor_scalar(V("ones"), fr, 0.0, None, A.is_ge), "k_c")
-    inc(v.tensor_scalar(V("rep", r=16), V("fri", r=16), col(1, 16), None, A.is_equal), "k_c")
-    inc(v.tensor_scalar(V("sel"), V("fr", 0, 16), col(1), None, A.is_equal), "k_c")
-    inc(v.tensor_scalar(V("selm"), V("fr", 0, 16), col(1), -16.0, A.is_equal, A.mult), "k_c")
-    inc(v.tensor_scalar(V("selr"), V("fr", 0, 16), col(1), col(2), A.is_equal, A.mult), "k_c")
-    inc(v.tensor_scalar(V("seln"), V("fr", 0, 16), col(1), -1.0, A.is_equal, A.mult), "k_c")
+    inc(ts(V("bo"), V("frr"), col(0), None, A.is_equal), "k_bo")
+    inc(ts(V("t1"), V("fri"), col(1), -1.0, A.is_le, A.mult), "k_bo")
+    inc(ts(V("ones"), fr, 0.0, None, A.is_ge), "k_c")
+    inc(ts(V("rep", r=16), V("fri", r=16), col(1, 16), None, A.is_equal), "k_c")
+    inc(ts(V("sel"), V("fr", 0, 16), col(1), None, A.is_equal), "k_c")
+    inc(ts(V("selm"), V("fr", 0, 16), col(1), -16.0, A.is_equal, A.mult), "k_c")
+    inc(ts(V("selr"), V("fr", 0, 16), col(1), col(2), A.is_equal, A.mult), "k_c")
+    inc(ts(V("seln"), V("fr", 0, 16), col(1), -1.0, A.is_equal, A.mult), "k_c")
     wv("k_bo")
-    inc(v.tensor_tensor(V("nt"), V("bo"), V("t1"), A.mult), "k_c")
-    inc(v.tensor_scalar(V("zz"), V("fr"), col(3), None, A.is_equal), "k_c")
-    inc(v.tensor_copy(V("iob"), fr), "k_c")
-    inc(v.memset(V("big"), 2.0 ** 99), "bg0")
-    inc(v.memset(T.win[:, 0:1], 0.0), "win0")
-    inc(v.memset(T.win[:, 129:130], 0.0), "win0")
-    wv("bg0")
-    inc(v.tensor_scalar(T.tw[:, 0:4], V("big"), -2.0, None, A.mult), "tws")
-    for k in range(2):
-        inc(v.tensor_scalar(T["run%d" % k][:, 0:4], V("big"), -2.0, None, A.mult), "rus")
-    inc(v.tensor_copy(T.rx[:, q * W + 76:q * W + 80], V("fr", 0, 4)), "pad")
+    inc(tt(V("nt"), V("bo"), V("t1"), A.mult), "k_c")
+    wa("bg", "io1")
+    for j in range(4):
+        inc(s_.activation(T[N("mark", h)][:, 512 * j:512 * j + 512], V("one"), F.Identity, bias=V("bgc", 0, 1), scale=0.0), N("mrk", h))
+    wv("ldr")
+    inc(ts(V("eri", r=1), T.erow[:], 15, None, A.bitwise_and), "eri")
     wv("lde")
     inc(v.tensor_copy(V("endf", r=16), T.endw[:]), "endf")
-    wv("ldr")
-    inc(v.tensor_scalar(V("eri", r=1), T.erow[:], 15, None, A.bitwise_and), "eri")
-    wp("k_c", "endf")
-    inc(mm(T.ps5[:, 0:32], V("rep", r=16), V("endf", r=16), True, True), "p_e")
-    wv("ldi")
-    inc(v.tensor_scalar(V("part"), T.v[:], 13, None, A.arith_shift_right), "part")
     wv("eri")
     inc(v.tensor_copy(V("erh", r=1), V("eri", r=1)), "erh")
+    wp("k_c", "endf")
+    inc(mm(T.ps5[:, 0:32], V("rep", r=16), V("endf", r=16), True, True), "p_e")
+
+    def spread(ks):
+        wp("erh")
+        for k in ks:
+            x = mm(T.ps6[:, 16 * k:16 * k + 16], V("ones", r=1), V("erh", k, 192, 12, 1), True, True)
+        return x
+
+    spread(range(6))
+    wv("ldi")
+    inc(ts(V("part"), T.v[:], 13, None, A.arith_shift_right), "part")
+    inc(ts(V("oli", r=16), T.v[0:16, :], 127, None, A.bitwise_and), "oli")
     wv("part", "k_c")
-    inc(v.tensor_scalar(V("o4"), V("part"), col(0), None, A.is_equal), "o4")
-    inc(v.tensor_scalar(V("oli", r=16), T.v[0:16, :], 127, None, A.bitwise_and), "oli")
+    inc(ts(V("o4"), V("part"), col(0), None, A.is_equal), "o4")
     wv("o4")
     inc(v.tensor_tensor_scan(V("ic"), V("ones"), V("o4"), 0.0, A.mult, A.add), "ic")
-    inc(v.tensor_scalar(V("ohi", r=16), T.v[0:16, :], 8064, None, A.bitwise_and), "oli")
+    inc(ts(V("ohi", r=16), T.v[0:16, :], 8064, None, A.bitwise_and), "oli")
     wp("o4", "k_bo")
     mm(T.ps0[:, 0:128], V("nt"), V("o4"), True, False)
     wp("ic")
@@ -212,22 +211,19 @@ def rank_program(g, core, T, topo):
     mm(T.ps3[:, 0:128], V("nt"), V("o4"), True, False)
     inc(mm(T.ps3[:, 0:128], V("bo"), V("ic"), False, True), "s4b")
     wv("oli")
-    inc(v.tensor_scalar(V("ol", r=16), V("oli", r=16), 4.0, None, A.add), "olh")
+    inc(ts(V("ol", r=16), V("oli", r=16), 4.0, None, A.add), "olh")
     inc(v.tensor_copy(V("oh", r=16), V("ohi", r=16)), "olh")
     wp("olh")
     mm(T.ps7[:, 0:16], V("ol", r=16), V("sel", r=16), True, True)
     mm(T.ps7[:, 16:32], V("oh", r=16), V("sel", r=16), True, True)
     mm(T.ps7[:, 32:48], V("ol", r=16), V("seln", r=16), True, True)
     inc(mm(T.ps7[:, 48:64], V("oh", r=16), V("seln", r=16), True, True), "p_ol")
-    wp("erh")
-    for k in range(12):
-        x = mm(T.ps6[:, 16 * k:16 * k + 16], V("ones", r=1), V("erh", k, 192, 12, 1), True, True)
-    inc(x, "p_eb")
+    inc(spread(range(6, 12)), "p_eb")
     wv("s4")
-    inc(v.tensor_scalar(V("h4i"), T.ps0[:, 0:128], -7.5, 1.0 / 16, A.add, A.mult), "h4i")
-    inc(v.tensor_tensor(V("m4"), T.ps0[:, 0:128], V("o4"), A.mult), "m4")
+    inc(ts(V("h4i"), T.ps0[:, 0:128], -7.5, 1.0 / 16, A.add, A.mult), "h4i")
+    inc(tt(V("m4"), T.ps0[:, 0:128], V("o4"), A.mult), "m4")
     wv("h4i")
-    inc(v.tensor_tensor(V("h4"), V("h4i"), V("o4"), A.mult), "h4")
+    inc(tt(V("h4"), V("h4i"), V("o4"), A.mult), "h4")
     wa("s4b", "win0")
     inc(s_.activation(T.win[:, 1:129], T.ps3[:, 0:128], F.Identity), "win")
     wp("m4", "h4")
@@ -236,141 +232,156 @@ def rank_program(g, core, T, topo):
     mm(T.ps1[:, 0:16], V("h4"), V("selm"), False, True)
     inc(mm(T.ps1[:, 16:32], V("h4"), V("sel"), True, True), "p_l3")
     wv("p_e")
-    inc(v.tensor_scalar(V("eci"), T.ps5[:, c0(q):c0(q) + 12], 8.5 - 2048.0 * q, 1.0 / 16, A.add, A.mult), "eci")
+    inc(ts(V("eci"), T.ps5[:, c0(q):c0(q) + 12], 8.5 - 2048.0 * q, 1.0 / 16, A.add, A.mult), "eci")
+    inc(v.tensor_copy(V("iob"), fr), "k_i")
+    wv("eci")
+    inc(ts(V("ecl"), V("eci"), 0.0, 129.0, A.max, A.min), "ecl")
     wv("p_ol")
     inc(v.tensor_copy(V("pay"), T.ps7[:, 0:64]), "pay")
-    wv("eci")
-    inc(v.tensor_scalar(V("ecl"), V("eci"), 0.0, 129.0, A.max, A.min), "ecl")
+    wv("p_eb")
+    inc(ts(V("mk"), T.ps6[:, 0:192], col(1), None, A.is_equal), "mk")
     wv("p_l3")
     inc(v.tensor_copy(V("l3"), T.ps1[:, 0:32]), "l3")
-    wv("p_eb")
-    inc(v.tensor_scalar(V("mk"), T.ps6[:, 0:192], col(1), None, A.is_equal), "mk")
     wv("ecl", "win", "mk", "win0")
-    inc(v.tensor_tensor(V("yy"), T.win[:, 0:130].indirect(V("ecl")), V("mk"), A.mult), "yy")
-    ev, od = list(range(0, 16, 2)), list(range(1, 16, 2))
-    wa("l3", "pay", "k_c")
-    for i in od:
-        inc(s_.activation(V("ta", 32 * i, 32 * i + 32), V("iob", 0, 32), F.Abs, bias=V("l3", 16 + i, 17 + i), scale=-1.0), "ta")
+    inc(tt(V("yy"), T.win[:, 0:130].indirect(V("ecl")), V("mk"), A.mult), "yy")
+    inc(ts(V("zz"), V("fr"), col(3), None, A.is_equal), "k_z")
+    ev = [0, 2, 4, 6, 8, 10, 12]
+    od = [i for i in range(16) if i not in ev]
+    wa("l3", "pay", "k_i")
+    for k, i in enumerate(od):
+        inc(s_.activation(V("ta", 32 * k, 32 * k + 32), V("iob", 0, 32), F.Abs, bias=V("l3", 16 + i, 17 + i), scale=-1.0), "ta")
     wa("ta")
-    for i in od:
+    for k, i in enumerate(od):
         for d in range(2):
-            inc(s_.activation(T.bb[:, 64 * i + 32 * d:64 * i + 32 * d + 32], V("ta", 32 * i, 32 * i + 32), F.Relu,
+            inc(s_.activation(T.bb[:, 64 * i + 32 * d:64 * i + 32 * d + 32], V("ta", 32 * k, 32 * k + 32), F.Relu,
                               bias=V("pay", 16 * d + i, 16 * d + i + 1), scale=V("pay", 32 + 16 * d + i, 33 + 16 * d + i)), "c%d" % i)
-    wv("l3", "pay", "k_c")
-    for i in ev + od:
-        inc(v.tensor_scalar(T.aa[:, 128 * i:128 * i + 128], V("iob"), V("l3", i, i + 1), None, A.is_equal), "c%d" % i)
+    for j in range(4):
+        inc(s_.activation(T[N("mark", f)][:, 512 * j:512 * j + 512], V("one"), F.Identity, bias=V("bgc", 0, 1), scale=0.0), N("mrk", f))
+    wp("yy", "k_z")
+    for b in range(16):
+        x = mm(T.ps4[:, 0:12], V("zz", 15 - b, 143 - b), V("yy", b, 192, 16), b == 0, b == 15)
+    inc(x, "p_pp")
+    o = q * W
+    inc(v.tensor_copy(T.rx[:, o + 76:o + 80], V("fr", 0, 4)), "pad")
+    wv("l3", "pay", "k_i")
+    order = ev + od
+    for n, i in enumerate(order):
+        inc(ts(T.aa[:, 128 * i:128 * i + 128], V("iob"), V("l3", i, i + 1), None, A.is_equal), "c%d" % i)
         if i in ev:
             for d in range(2):
-                inc(v.tensor_scalar(T.bb[:, 64 * i + 32 * d:64 * i + 32 * d + 32], V("iob", 0, 32), V("l3", 16 + i, 17 + i),
-                                    V("pay", 16 * d + i, 16 * d + i + 1), A.is_equal, A.mult), "c%d" % i)
-    wp("yy")
-    for b in range(16):
-        mm(T.ps2[:, 64:76], V("zz", 15 - b, 143 - b), V("yy", b, 192, 16), b == 0, b == 15)
-    order = ev + od
+                inc(ts(T.bb[:, 64 * i + 32 * d:64 * i + 32 * d + 32], V("iob", 0, 32), V("l3", 16 + i, 17 + i),
+                       V("pay", 16 * d + i, 16 * d + i + 1), A.is_equal, A.mult), "c%d" % i)
+        if n == 10:
+            wv("p_pp")
+            inc(v.tensor_copy(T.rx[:, o + 64:o + 76], T.ps4[:, 0:12]), "ptx")
     for i in order:
         wp("c%d" % i)
         x = mm(T.ps2[:, 0:64], T.aa[:, 128 * i:128 * i + 128], T.bb[:, 64 * i:64 * i + 64], i == order[0], i == order[-1])
     inc(x, "p_x")
     wv("p_x")
-    inc(v.tensor_copy(T.rx[:, q * W:q * W + 76], T.ps2[:, 0:76]), "tx")
-    own = T.rx[:, q * W:(q + 1) * W]
-    others = [cores[r] for r in near if r != q]
-    to = others + [c for c in gates[h] if T.rank_of(c) is None]
-    wt("g", g, "tx", "pad")
-    g.remote_dma_fused([RemoteDMATransfer(srcs=[own], dsts=[own] * len(to), dst_ids=[did(c) for c in to],
-                                          dma_engine_mask=topo.mask(core, to[0]), remote_sem=S.nx)], local_sem=S.ls)
+    inc(v.tensor_copy(T.rx[:, o:o + 64], T.ps2[:, 0:64]), "tx")
+    to = [c for c in gates if c != core] + [cores[r] for r in near if r != q and cores[r] not in gates]
+    full = topo.mask(core, to[0])
+    t = T.rx[:, o:o + W]
+    wt("g", g, "ptx", "pad", "tx")
+    g.remote_dma_fused([RemoteDMATransfer(srcs=[t], dsts=[t] * len(to), dst_ids=[did(c) for c in to], dma_engine_mask=full,
+                                          remote_sem=S.nx)], local_sem=S.ls)
+    g.sem_inc(S.go, 1)
+    wt("sy", sy, "go")
+    load(1)
     nls = 16
-    cnt["nx"] = 16 * (len(near) - 1)
-    cnt["fx"] = 8
     if gate:
         wt("g", g, "nx")
-        a = topo.addr(farcore)
-        g.remote_dma(tiles, tiles, S.fx, S.ls, a[1], a[0], topo.mask(core, farcore))
+        pass_on()
         nls += 8
-    inc(v.tensor_scalar(V("big", 1, 2), V("big", 0, 1), 4.0, None, A.mult), "bg")
-    inc(v.tensor_scalar(V("s_o"), V("fri"), col(1), col(6), A.is_equal, A.mult), "k_s")
-    inc(v.tensor_scalar(V("s_a"), V("fri"), col(4), col(6), A.is_equal, A.mult), "k_s")
-    inc(v.tensor_scalar(V("s_b"), V("fri"), col(5), col(7), A.is_equal, A.mult), "k_d")
-    inc(v.tensor_scalar(V("bq"), T.ps5[:, 0:32], -1023.5, 1.0 / 2048, A.add, A.mult), "bq")
+    inc(ts(col(4), ii, 1.0, None, A.add), "k_cg")
+    inc(ts(col(5), ii, -15.0, None, A.add), "k_cg")
+    inc(ts(col(6), ri, float(q), None, A.is_equal), "k_cg")
+    inc(ts(col(7), ri, float(q), -1.0, A.is_equal, A.mult), "k_cg")
+    inc(ts(V("bq"), T.ps5[:, 0:32], -1023.5, 1.0 / 2048, A.add, A.mult), "bq")
     inc(v.memset(V("src"), -2.0 ** 99), "src0")
-    wv("k_s")
-    inc(v.tensor_tensor(V("s_d"), V("s_o"), V("s_a"), A.subtract), "k_d")
+    wv("k_cg")
+    inc(ts(V("s_o"), V("fri"), col(1), col(6), A.is_equal, A.mult), "k_s")
+    inc(ts(V("s_a"), V("fri"), col(4), col(6), A.is_equal, A.mult), "k_s")
+    inc(ts(V("s_b"), V("fri"), col(5), col(7), A.is_equal, A.mult), "k_d")
     wv("bq")
-    inc(v.tensor_scalar(V("b0i"), V("bq", 0, 20), 0.0, 4.0, A.max, A.min), "bi")
-    inc(v.tensor_scalar(V("b1i"), V("bq", 12, 32), -4.0, 0.0, A.add, A.max), "bi")
-    wv("src0")
-    inc(v.tensor_scalar(V("src"), V("src"), 2.0, None, A.mult), "src")
+    inc(ts(V("b0i"), V("bq", 0, 20), 0.0, 4.0, A.max, A.min), "bi")
+    inc(ts(V("b1i"), V("bq", 12, 32), -4.0, 0.0, A.add, A.max), "bi")
+    wv("k_s")
+    inc(tt(V("s_d"), V("s_o"), V("s_a"), A.subtract), "k_d")
     wv("bi")
-    inc(v.tensor_scalar(V("base0"), V("b0i"), 512.0, None, A.mult), "bs")
-    inc(v.tensor_scalar(V("base1"), V("b1i"), 4.0, 512.0, A.min, A.mult), "bs")
-    wa("bg", "iom")
-    inc(s_.activation(fmark[:, 0:HB], nmark[:, 0:HB], F.Copy, scale=V("big", 1, 2)), "mrk")
-    wa("mrk")
-    inc(s_.activation(nmark[:, 0:HB], nmark[:, 0:HB], F.Copy, scale=V("big", 1, 2)), "mrk2")
+    inc(ts(V("base0"), V("b0i"), 512.0, None, A.mult), "bs")
+    inc(ts(V("base1"), V("b1i"), 4.0, 512.0, A.min, A.mult), "bs")
+    wv("src0")
+    inc(ts(V("src"), V("src"), 2.0, None, A.mult), "src")
+    inc(ts(T.tw[:, 0:4], V("big"), -2.0, None, A.mult), "tws")
+    for k in range(2):
+        inc(ts(T[N("run", k)][:, 0:4], V("big"), -2.0, None, A.mult), "rus")
+    inc(v.tensor_copy(V("erf", r=1), T.erow[:]), "erf")
+    inc(v.memset(V("onef", r=1), 1.0), "erf")
 
     psx = {h: T.ps0, f: T.ps1}
     psp = {h: T.ps3, f: T.ps4}
     psd = {h: T.ps5, f: T.ps6}
 
-    def N(n, k):
-        return "%s%d" % (n, k)
-
-    def pe_half(k, arrived):
-        ps = psx[k]
-        bs = N("base", k)
-        P, D = psp[k], psd[k]
+    def pe_base(k):
         wp("k_s", "k_d", "bs")
-        mm(P[:, 0:20], V("s_o"), V(bs), True, False)
-        mm(D[:, 0:20], V("s_d"), V(bs), True, False)
-        mm(D[:, 1:20], V("s_b"), V(bs, 0, 19), False, False)
-        wp(arrived)
-        if k == h:
-            wp("tx")
+        bs = N("base", k)
+        mm(psp[k][:, 0:20], V("s_o"), V(bs), True, False)
+        mm(psd[k][:, 0:20], V("s_d"), V(bs), True, False)
+        mm(psd[k][:, 1:20], V("s_b"), V(bs, 0, 19), False, False)
+
+    def pe_lists(k):
         for j, s in enumerate(ranks[k]):
-            mm(ps[:, 32 * j:32 * j + 32], V("s_o"), T.rx[:, s * W:s * W + 32], True, False)
-            x = mm(ps[:, 32 * j:32 * j + 32], V("s_o"), T.rx[:, s * W + 32:s * W + 64], False, True)
+            p = psx[k][:, 32 * j:32 * j + 32]
+            mm(p, V("s_o"), T.rx[:, s * W:s * W + 32], True, False)
+            x = mm(p, V("s_o"), T.rx[:, s * W + 32:s * W + 64], False, True)
         inc(x, N("p_xl", k))
+
+    def pe_borders(k):
+        P, D = psp[k], psd[k]
         last = ranks[k][-1]
         for s in ranks[k]:
             o = c0(s) - 12 * k
-            t = T.rx[:, s * W + 64:s * W + 76]
+            b = s * W + 64
             w = min(12, 19 - o)
-            x1 = mm(P[:, o:o + 12], V("s_o"), t, False, s == last)
-            mm(D[:, o:o + 12], V("s_d"), t, False, False)
-            x2 = mm(D[:, o + 1:o + 1 + w], V("s_b"), T.rx[:, s * W + 64:s * W + 64 + w], False, s == last)
+            x1 = mm(P[:, o:o + 12], V("s_o"), T.rx[:, b:b + 12], False, s == last)
+            mm(D[:, o:o + 12], V("s_d"), T.rx[:, b:b + 12], False, False)
+            x2 = mm(D[:, o + 1:o + 1 + w], V("s_b"), T.rx[:, b:b + w], False, s == last)
         inc(x1, N("p_p", k))
         inc(x2, N("p_p", k))
 
-    def gathers(k):
-        for j in range(4):
-            wa(N("xo", k), "ldt", "tws")
-            inc(s_.activation(T[N("gd", k)][:, 512 * j:512 * j + 512],
-                              T.tw[:].indirect(V(N("xo", k), 32 * j, 32 * j + 32)), F.Copy), N("g" + "abcd"[j], k))
+    def gather(k, j):
+        wa(N("xo", k), "ldt", "tws")
+        inc(s_.activation(T[N("gd", k)][:, 512 * j:512 * j + 512], T.tw[:].indirect(V(N("xo", k), 32 * j, 32 * j + 32)), F.Copy),
+            N("g" + "abcd"[j], k))
 
-    def lists(k):
+    def offsets(k):
+        wv(N("p_xl", k))
+        inc(v.tensor_copy(V(N("xo", k)), psx[k][:, 0:128]), N("xo", k))
+
+    def borders(k):
         def n(x):
             return V(N(x, k))
-        wv(N("p_xl", k))
-        inc(v.tensor_copy(n("xo"), psx[k][:, 0:128]), N("xo", k))
         wv(N("p_p", k), "iom")
-        inc(v.tensor_scalar(n("nd"), psd[k][:, 0:20], 0.0, None, A.is_gt), N("nd", k))
-        inc(v.tensor_tensor(n("pt"), psp[k][:, 0:20], V("trash"), A.subtract), N("pt", k))
+        inc(ts(n("nd"), psd[k][:, 0:20], 0.0, None, A.is_gt), N("nd", k))
+        inc(tt(n("pt"), psp[k][:, 0:20], V("trash"), A.subtract), N("pt", k))
         wv(N("nd", k), N("pt", k))
-        inc(v.tensor_tensor(n("sa"), n("nd"), n("pt"), A.mult), N("sa", k))
-        inc(v.tensor_tensor(n("pk"), psp[k][:, 0:20], n("nd"), A.mult), N("pk", k))
+        inc(tt(n("sa"), n("nd"), n("pt"), A.mult), N("sa", k))
+        inc(tt(n("pk"), psp[k][:, 0:20], n("nd"), A.mult), N("pk", k))
         wv(N("sa", k))
-        inc(v.tensor_tensor(n("sb"), n("sa"), V("trash"), A.add), N("sb", k))
+        inc(tt(n("sb"), n("sa"), V("trash"), A.add), N("sb", k))
         wv(N("pk", k))
         inc(v.tensor_copy(n("po"), n("pk")), N("po", k))
         wv(N("sb", k))
         inc(v.tensor_copy(n("sc"), n("sb")), N("sc", k))
-        wv(N("sc", k), "src", "mrk", "mrk2")
+        wv(N("sc", k), "src", N("mrk", k))
         inc(v.tensor_copy(T[N("mark", k)][:].indirect(n("sc")), V("src")), N("sct", k))
 
-    def scans(k):
+    def scans(k, js):
         run = T[N("run", k)]
         wv(N("sct", k), "rus")
-        for j in range(4):
+        for j in js:
             wv(N("g" + "abcd"[j], k))
             if j:
                 wv(N("r" + "abcd"[j - 1], k))
@@ -378,45 +389,64 @@ def rank_program(g, core, T, topo):
                                      T[N("gd", k)][:, 512 * j:512 * j + 512], run[:, 3 + 512 * j:4 + 512 * j], A.min, A.max),
                 N("r" + "abcd"[j], k))
 
-    def picks(k):
-        e = 12 if k == 0 else 0
-        o = 0 if k == 0 else 8
-        names = [N("r" + c, k) for c in "abcd"]
-        wa(N("po", k), "rus", *names)
-        inc(s_.activation(T[N("pick", k)][:, 16 * o:16 * o + 192],
-                          T[N("run", k)][:, 3:HB + 4].indirect(V(N("po", k), o, o + 12)), F.Copy), N("pik", k))
-        wv(N("po", k), *names)
-        inc(v.tensor_copy(T[N("pick", k)][:, 16 * e:16 * e + 128],
-                          T[N("run", k)][:, 3:HB + 4].indirect(V(N("po", k), e, e + 8))), N("pib", k))
+    def pick(k, both):
+        o, n = ((12, 8) if both else (0, 12)) if k == 0 else ((0, 8) if both else (8, 12))
+        wt("v" if both else "a", v if both else s_, N("po", k), "rus", *[N("r" + c, k) for c in "abcd"])
+        out = T[N("pick", k)][:, 16 * o:16 * (o + n)]
+        i = T[N("run", k)][:, 3:HB + 4].indirect(V(N("po", k), o, o + n))
+        inc(v.tensor_copy(out, i) if both else s_.activation(out, i, F.Copy), N("pib" if both else "pik", k))
 
     def piece(d):
-        if d in (3, 4):
-            return T.cm[:, 64 * (d - 3):64 * (d - 2)]
-        return T.pick0[:, 64 * d:64 * d + 64] if d < 3 else T.pick1[:, 64 * (d - 3):64 * (d - 2)]
+        return T.pick0[:, 64 * d:64 * (d + 1)] if d < 4 else T.pick1[:, 64 * (d - 3):64 * (d - 2)]
 
-    pe_half(h, "nx")
-    lists(h)
-    gathers(h)
-    inc(v.tensor_copy(V("erf", r=1), T.erow[:]), "erf")
-    inc(v.memset(V("onef", r=1), 1.0), "erf")
+    pe_base(h)
+    pe_base(f)
     lo = 4 * q - 1 - c0(q)
     wp("erf")
     for k in range(5):
         if lo + k >= 0:
             x = mm(T.ps7[:, 16 * k:16 * k + 16], V("onef", r=1), V("erf", lo + k, 192, 12, 1), True, True)
     inc(x, "p_z")
-    scans(h)
-    picks(h)
-    done = [d for d in near if d not in (3, 4)]
-    rest = [d for d in near if d in (3, 4)][0]
-    send = [d for d in done if d != q]
-    full = topo.mask(core, others[0])
-    mine = T.nl[:, 64 * near.index(q):64 * near.index(q) + 64]
-    wt("g", g, N("pik", h))
+    wp("nx", "tx", "ptx")
+    pe_lists(h)
+    pe_borders(h)
+    offsets(h)
+    for j in range(4):
+        gather(h, j)
+    borders(h)
+    wp("fx")
+    pe_lists(f)
+    pe_borders(f)
+    scans(h, range(3))
+    offsets(f)
+    scans(h, range(3, 4))
+    pick(h, True)
+    for j in range(4):
+        gather(f, j)
+    borders(f)
+    scans(f, range(4))
+    pick(f, True)
+    pick(f, False)
+    pick(h, False)
+    fb, nb = (4, 3) if h == 0 else (3, 4)
+    wv("pib0", "pib1")
+    for d, sem in ((fb, "cmf"), (nb, "cmn")):
+        a, b = T.pick0[:, 64 * d:64 * d + 64], T.pick1[:, 64 * (d - 3):64 * (d - 2)]
+        inc(tt(piece(d), a, b, A.max), sem)
     ms = split(full, 4)
-    g.remote_dma_fused([RemoteDMATransfer(srcs=[piece(d)], dsts=[mine], dst_ids=[did(cores[d])], dma_engine_mask=ms[k],
-                                          remote_sem=S.ne2) for k, d in enumerate(send)], local_sem=S.ls)
-    nls += 4 * len(send)
+    wt("g", g, "cmf", N("pik", f))
+    tr = [RemoteDMATransfer(srcs=[piece(far[k])], dsts=[T.gl[:, 64 * me:64 * me + 64]], dst_ids=[did(c)], dma_engine_mask=ms[k],
+                            remote_sem=S.gx) for k, c in enumerate(gates) if c != core]
+    g.remote_dma_fused(tr, local_sem=S.ls)
+    wt("g", g, "cmn", N("pik", h))
+    g.remote_dma_fused([RemoteDMATransfer(srcs=[piece(r)], dsts=[T.nl[:, 64 * me:64 * me + 64]], dst_ids=[did(cores[r])],
+                                          dma_engine_mask=ms[3 - k], remote_sem=S.ne2) for k, r in enumerate([r for r in near if r != q])],
+                       local_sem=S.ls)
+    nls += 4 * len(tr) + 4 * n3
+    if gate:
+        g.wait_ge(S.gx, 4 * n3)
+        fold([piece(fd) if r == q else T.gl[:, 64 * k:64 * k + 64] for k, r in enumerate(near)])
+        nls += 8
     b0 = 0
     if lo < 0:
         inc(v.memset(V("eb", 0, 16), 0.0), "ebz")
@@ -425,50 +455,23 @@ def rank_program(g, core, T, topo):
     wv("p_z")
     inc(v.tensor_copy(V("eb", b0, 80), T.ps7[:, b0:80]), "eb")
     wv("eb")
-    inc(v.tensor_tensor(V("ne"), V("eb", 16, 80), V("eb", 15, 79), A.is_gt), "ne")
+    inc(tt(V("ne"), V("eb", 16, 80), V("eb", 15, 79), A.is_gt), "ne")
     wv("ne")
-    inc(v.tensor_scalar(V("ze"), V("ne"), -2.0 ** 99, 0.0, A.mult, A.add), "ze")
+    inc(ts(V("ze"), V("ne"), -2.0 ** 99, 0.0, A.mult, A.add), "ze")
     wv("ze")
-    inc(v.tensor_scalar(V("zf"), V("ze"), 2.0, None, A.mult), "zf")
-    pe_half(f, "fx")
-    lists(f)
-    gathers(f)
-    scans(f)
-    picks(f)
-    wv("pib0", "pib1")
-    inc(v.tensor_tensor(T.cm[:], T.pick0[:, 192:320], T.pick1[:, 0:128], A.max), "cm")
-    wt("g", g, "cm", N("pik", f))
-    tr = []
-    for k, c in enumerate(gates[h]):
-        if c != core:
-            tr.append(RemoteDMATransfer(srcs=[piece(ranks[f][k])], dsts=[T.gl[:, 64 * near.index(q):64 * near.index(q) + 64]],
-                                        dst_ids=[did(c)], dma_engine_mask=ms[k], remote_sem=S.gx))
-    g.remote_dma_fused(tr, local_sem=S.ls)
-    nls += 4 * len(tr)
-    if rest != q:
-        a = topo.addr(cores[rest])
-        g.remote_dma(mine, piece(rest), S.ne2, S.ls, a[1], a[0], full)
-        nls += 16
-    if gate:
-        g.wait_ge(S.gx, 4 * (len(near) - 1))
-        g.remote_dma_fused([RemoteDMATransfer(srcs=[piece(farrank) if r == q else T.gl[:, 64 * k:64 * k + 64] for k, r in enumerate(near)],
-                                              dsts=[T.fl[:]], dst_ids=[did(farcore)], dma_engine_mask=topo.mask(core, farcore),
-                                              remote_sem=S.ff, alu_op=2)], local_sem=S.ls)
-        nls += 8
-    cnt["ne2"] = (4 if q in done else 16) * (len(near) - 1)
-    cnt["ff"] = 8
-    wv("cm", N("pik", h), "zf")
-    inc(v.tensor_tensor(V("ya"), piece(q), V("zf"), A.max), "ya")
+    inc(ts(V("zf"), V("ze"), 2.0, None, A.mult), "zf")
+    wv("cmn", N("pik", h), "zf")
+    inc(tt(V("ya"), piece(q), V("zf"), A.max), "ya")
     last = "ya"
     wv("ne2")
     names = ["yb", "yc", "yd"]
     for k, r in enumerate([r for r in near if r != q]):
         wv(last)
         j = near.index(r)
-        inc(v.tensor_tensor(V(names[k]), V(last), T.nl[:, 64 * j:64 * j + 64], A.max), names[k])
+        inc(tt(V(names[k]), V(last), T.nl[:, 64 * j:64 * j + 64], A.max), names[k])
         last = names[k]
     wv(last, "ff")
-    inc(v.tensor_tensor(V("ye"), V(last), T.fl[:], A.max), "ye")
+    inc(tt(V("ye"), V(last), T.fl[:], A.max), "ye")
     wt("sy", sy, "ye")
     sy.dma_start(T.y[:], V("ye")).then_inc(S.st, 16)
     sy.wait_ge(S.st, 16)

@@ -3,7 +3,8 @@ from concourse.mybir import dt, AluOpType, AxisListType, ActivationFunctionType
 
 W = 80
 HB = 2048
-CUT = (0, 7168, 8192)
+B0 = 512
+CUT = (0, 6656, 8192)
 
 SCRATCH = {
     "v": ("sbuf", [128, 128], "int32"), "endw": ("sbuf", [16, 32], "int32"), "erow": ("sbuf", [1, 192], "int32"),
@@ -12,19 +13,19 @@ SCRATCH = {
     "nl": ("sbuf", [128, 256], "float32"), "gl": ("sbuf", [128, 256], "float32"), "fl": ("sbuf", [128, 64], "float32"),
 }
 for _h in range(2):
-    for _n, _w, _d in (("mark", 2496, "bfloat16"), ("gd", HB, "float32"), ("run", HB + 4, "float32"), ("pick", 320, "float32")):
+    for _n, _w, _d in (("mark", B0 + HB + 16, "bfloat16"), ("gd", HB, "float32"), ("run", B0 + HB + 4, "float32"), ("pick", 320, "float32")):
         SCRATCH["%s%d" % (_n, _h)] = ("sbuf", [128, _w], _d)
 for _b in range(8):
     SCRATCH["ps%d" % _b] = ("psum", [128, 512], "float32")
 LAY = {}
 for _a, _d, _l in (
-    ("ai", "int32", "pi 4 ri 4 ii 4 fr 144 frr 128 fri 128 part 128 h4i 128 oli 128 ohi 128 eri 192 eci 12 bq 32 b0i 20 b1i 20"),
-    ("ah", "float16", "bo 128 t1 128 nt 128 sel 16 selm 16 selr 16 seln 16 zz 144 ones 128 o4 128 ic 128 m4 128 h4 128 "
-                      "ol 128 oh 128 erh 192 mk 192 yy 192 s_o 128 s_a 128 s_d 128 s_b 128 base0 20 base1 20"),
+    ("ai", "int32", "pi 4 ri 4 ii 4 fr 144 frr 128 fri 128 part 128 oli 128 ohi 128 eri 192 eci 12 bq 32 b0i 20 b1i 20"),
+    ("ah", "float16", "c2 128 sel 16 selm 16 seln 16 zz 144 m4 128 hh 128 ol 128 oh 128 mk 192 yy 192 "
+                      "s_o 128 s_a 128 s_d 128 s_b 128 base0 20 base1 20 bass0 20 bass1 20"),
     ("af", "float32", "cf 8 rep 128 onef 128 big 4 bgc 4 l3 32 pay 64 endf 32 erf 192 trash 20 eb 80 ne 64 ze 64 zf 64 "
-                      "ya 64 yb 64 yc 64 yd 64 ye 64 nd0 20 nd1 20 pt0 20 pt1 20 sa0 20 sa1 20 sb0 20 sb1 20 pk0 20 pk1 20"),
-    ("ab", "bfloat16", "iob 128 ta 512 src 320 one 512"),
-    ("au", "uint16", "xo0 128 xo1 128 sc0 20 sc1 20 po0 20 po1 20 ecl 12"),
+                      "ya 64 yb 64 yc 64 yd 64 ye 64 dk0 20 dk1 20 sa0 20 sa1 20 sb0 20 sb1 20"),
+    ("ab", "bfloat16", "selr 16 iob 128 bo 128 nbo 128 nt 128 o4 128 ic 128 erh 192 erq 192 ta 512 src 320 one 512"),
+    ("au", "uint16", "xo0 128 xo1 128 sc0 20 sc1 20 ecl 12"),
 ):
     _o = 0
     _p = _l.split()
@@ -34,13 +35,13 @@ for _a, _d, _l in (
     SCRATCH[_a] = ("sbuf", [128, _o], _d)
 
 SEMAPHORES = ["ldi", "lde", "ldr", "ldt", "st", "nx", "fx", "ls", "ne2", "gx", "ff", "go",
-              "io", "io1", "iom", "k_ri", "k_cf", "k_cg", "k_fr", "k_bo", "k_c", "k_z", "k_i", "bg0", "bg", "tws", "rus",
-              "endf", "eri", "erh", "p_e", "eci", "ecl", "p_eb", "mk", "part", "o4", "ic", "s4", "s4b", "win0", "win",
-              "m4", "h4i", "h4", "oli", "olh", "p_ol", "pay", "p_l3", "l3", "ta", "yy", "p_pp", "p_x", "pad", "ptx", "tx",
-              "k_s", "k_d", "bq", "bi", "bs", "src0", "src", "erf", "p_z", "ebz", "eb", "ne", "ze", "zf", "mrk0", "mrk1",
-              "cmf", "cmn", "ya", "yb", "yc", "yd", "ye"] + ["c%d" % i for i in range(16)]
+              "io", "io1", "iom", "k_ri", "k_cf", "k_cg", "k_fr", "k_b", "k_c", "k_z", "k_i", "k_n", "k_t", "bg0", "bg", "tws", "rus",
+              "endf", "eri", "erh", "erq", "p_e", "eci", "ecl", "p_eb", "mk", "part", "o4", "ic", "s4", "s4b", "win0", "win",
+              "m4", "hh", "oli", "olh", "p_ol", "pay", "p_l3", "l3", "ta", "yy", "p_pp", "p_x", "ptx", "tx",
+              "k_s", "k_d", "bq", "bi", "bs", "bss", "src0", "src", "erf", "p_z", "ebz", "eb", "ne", "ze", "zf", "mrk0", "mrk1",
+              "cmf", "cmn", "pe", "pl", "pf", "pn", "ya", "yb", "yc", "yd", "ye"] + ["c%d" % i for i in range(16)]
 for _h in range(2):
-    SEMAPHORES += ["%s%d" % (n, _h) for n in ("p_xl", "p_p", "xo", "nd", "pt", "sa", "sb", "sc", "sct", "pk", "po",
+    SEMAPHORES += ["%s%d" % (n, _h) for n in ("p_xl", "p_p", "p_x0", "xp", "xo", "dk", "sa", "sb", "sc", "sct",
                                                "ga", "gb", "gc", "gd", "ra", "rb", "rc", "rd", "pik", "pib")]
 
 
@@ -87,7 +88,7 @@ def rank_program(g, core, T, topo):
     if q is None:
         g.wait_ge(S.nx, 16 * n3)
         pass_on()
-        g.wait_ge(S.gx, 4 * n3)
+        g.wait_ge(S.gx, 8 * n3)
         fold([T.gl[:, 64 * k:64 * k + 64] for k in range(len(near))])
         g.wait_ge(S.ls, 16)
         return
@@ -145,12 +146,14 @@ def rank_program(g, core, T, topo):
     inc(g.iota(V("pi", 0, 1), [[1, 1]], 0, 1), "io")
     inc(g.iota(V("fr"), [[1, 144]], 0, 0), "io")
     inc(g.iota(V("one"), [[0, 512]], 1, 0, allow_small_or_imprecise_dtypes=True), "io1")
-    inc(g.iota(V("trash"), [[16, 20]], HB + 1, 1, allow_small_or_imprecise_dtypes=True), "iom")
+    inc(g.iota(V("iob"), [[1, 128]], 0, 0, allow_small_or_imprecise_dtypes=True), "k_i")
+    inc(g.iota(V("trash"), [[16, 20]], 0, 1, allow_small_or_imprecise_dtypes=True), "iom")
     inc(v.memset(V("big"), 2.0 ** 99), "bg0")
     inc(v.memset(T.win[:, 0:1], 0.0), "win0")
     inc(v.memset(T.win[:, 129:130], 0.0), "win0")
     wv("bg0")
-    inc(ts(V("bgc"), V("big"), 4.0, None, A.mult), "bg")
+    inc(ts(V("bgc", 0, 1), V("big", 0, 1), 4.0, None, A.mult), "bg")
+    inc(ts(V("bgc", 1, 2), V("big", 0, 1), -2.0, None, A.mult), "bg")
     wv("io")
     ri, ii, fr = V("ri", 0, 1), V("ii", 0, 1), V("fr", 0, 128)
     inc(ts(ri, V("pi", 0, 1), 4, None, A.arith_shift_right), "k_ri")
@@ -167,44 +170,46 @@ def rank_program(g, core, T, topo):
     inc(ts(col(2), ri, 16.0, None, A.mult), "k_cf")
     inc(ts(col(3), ri, 16.0, 15.0, A.mult, A.add), "k_cf")
     wv("k_cf", "k_fr")
-    inc(ts(V("bo"), V("frr"), col(0), None, A.is_equal), "k_bo")
-    inc(ts(V("t1"), V("fri"), col(1), -1.0, A.is_le, A.mult), "k_bo")
-    inc(ts(V("ones"), fr, 0.0, None, A.is_ge), "k_c")
+    inc(ts(V("bo"), V("frr"), col(0), None, A.is_equal), "k_b")
+    wa("k_b")
+    inc(s_.activation(V("nbo"), V("bo"), F.Copy, scale=-1.0), "k_n")
     inc(ts(V("rep", r=16), V("fri", r=16), col(1, 16), None, A.is_equal), "k_c")
     inc(ts(V("sel"), V("fr", 0, 16), col(1), None, A.is_equal), "k_c")
     inc(ts(V("selm"), V("fr", 0, 16), col(1), -16.0, A.is_equal, A.mult), "k_c")
     inc(ts(V("selr"), V("fr", 0, 16), col(1), col(2), A.is_equal, A.mult), "k_c")
     inc(ts(V("seln"), V("fr", 0, 16), col(1), -1.0, A.is_equal, A.mult), "k_c")
-    wv("k_bo")
-    inc(tt(V("nt"), V("bo"), V("t1"), A.mult), "k_c")
-    wa("bg", "io1")
-    for j in range(4):
-        inc(s_.activation(T[N("mark", h)][:, 512 * j:512 * j + 512], V("one"), F.Identity, bias=V("bgc", 0, 1), scale=0.0), N("mrk", h))
+    inc(ts(V("c2"), fr, 0.0, -1536.0, A.mult, A.add), "k_c")
+    inc(ts(V("zz"), V("fr"), col(3), None, A.is_equal), "k_z")
+    wt("g", g, "k_n")
+    inc(g.affine_select(V("nt"), V("nbo"), [[-1, 128]], A.is_ge, 0.0, 0, 1), "k_t")
+
+    def marks(k, js):
+        wa("bg", "io1")
+        for j in js:
+            inc(s_.activation(T[N("mark", k)][:, B0 + 512 * j:B0 + 512 * j + 512], V("one"), F.Identity, bias=V("bgc", 0, 1), scale=0.0),
+                N("mrk", k))
+
+    marks(h, range(2))
     wv("ldr")
     inc(ts(V("eri", r=1), T.erow[:], 15, None, A.bitwise_and), "eri")
     wv("lde")
     inc(v.tensor_copy(V("endf", r=16), T.endw[:]), "endf")
     wv("eri")
     inc(v.tensor_copy(V("erh", r=1), V("eri", r=1)), "erh")
-    wp("k_c", "endf")
+    wp("k_b", "k_c", "endf", "io1")
     inc(mm(T.ps5[:, 0:32], V("rep", r=16), V("endf", r=16), True, True), "p_e")
-
-    def spread(ks):
-        wp("erh")
-        for k in ks:
-            x = mm(T.ps6[:, 16 * k:16 * k + 16], V("ones", r=1), V("erh", k, 192, 12, 1), True, True)
-        return x
-
-    spread(range(6))
+    wa("erh")
+    for k in range(12):
+        inc(s_.activation(V("erq", 16 * k, 16 * k + 16, r=1), V("erh", k, 192, 12, 1), F.Identity), "erq")
     wv("ldi")
     inc(ts(V("part"), T.v[:], 13, None, A.arith_shift_right), "part")
     inc(ts(V("oli", r=16), T.v[0:16, :], 127, None, A.bitwise_and), "oli")
-    wv("part", "k_c")
+    wv("part")
     inc(ts(V("o4"), V("part"), col(0), None, A.is_equal), "o4")
-    wv("o4")
-    inc(v.tensor_tensor_scan(V("ic"), V("ones"), V("o4"), 0.0, A.mult, A.add), "ic")
     inc(ts(V("ohi", r=16), T.v[0:16, :], 8064, None, A.bitwise_and), "oli")
-    wp("o4", "k_bo")
+    wv("o4", "io1")
+    inc(v.tensor_tensor_scan(V("ic"), V("one", 0, 128), V("o4"), 0.0, A.mult, A.add), "ic")
+    wp("o4", "k_t")
     mm(T.ps0[:, 0:128], V("nt"), V("o4"), True, False)
     wp("ic")
     inc(mm(T.ps0[:, 0:128], V("bo"), V("ic"), False, True), "s4")
@@ -213,38 +218,39 @@ def rank_program(g, core, T, topo):
     wv("oli")
     inc(ts(V("ol", r=16), V("oli", r=16), 4.0, None, A.add), "olh")
     inc(v.tensor_copy(V("oh", r=16), V("ohi", r=16)), "olh")
+    mm(T.ps1[:, 0:16], V("c2"), V("selm"), True, False)
+    mm(T.ps1[:, 0:16], V("o4"), V("selr"), False, False)
+    wp("erq")
+    inc(mm(T.ps6[:, 0:192], V("one", 0, 128, r=1), V("erq", r=1), True, True), "p_eb")
     wp("olh")
     mm(T.ps7[:, 0:16], V("ol", r=16), V("sel", r=16), True, True)
     mm(T.ps7[:, 16:32], V("oh", r=16), V("sel", r=16), True, True)
     mm(T.ps7[:, 32:48], V("ol", r=16), V("seln", r=16), True, True)
     inc(mm(T.ps7[:, 48:64], V("oh", r=16), V("seln", r=16), True, True), "p_ol")
-    inc(spread(range(6, 12)), "p_eb")
     wv("s4")
-    inc(ts(V("h4i"), T.ps0[:, 0:128], -7.5, 1.0 / 16, A.add, A.mult), "h4i")
     inc(tt(V("m4"), T.ps0[:, 0:128], V("o4"), A.mult), "m4")
-    wv("h4i")
-    inc(tt(V("h4"), V("h4i"), V("o4"), A.mult), "h4")
-    wa("s4b", "win0")
-    inc(s_.activation(T.win[:, 1:129], T.ps3[:, 0:128], F.Identity), "win")
-    wp("m4", "h4")
-    mm(T.ps1[:, 0:16], V("m4"), V("sel"), True, False)
-    mm(T.ps1[:, 0:16], V("o4"), V("selr"), False, False)
-    mm(T.ps1[:, 0:16], V("h4"), V("selm"), False, True)
-    inc(mm(T.ps1[:, 16:32], V("h4"), V("sel"), True, True), "p_l3")
     wv("p_e")
     inc(ts(V("eci"), T.ps5[:, c0(q):c0(q) + 12], 8.5 - 2048.0 * q, 1.0 / 16, A.add, A.mult), "eci")
-    inc(v.tensor_copy(V("iob"), fr), "k_i")
+    wv("m4")
+    inc(ts(V("hh"), V("m4"), 1.0 / 16, 1535.53125, A.mult, A.add), "hh")
+    wa("s4b", "win0")
+    inc(s_.activation(T.win[:, 1:129], T.ps3[:, 0:128], F.Identity), "win")
+    wp("m4")
+    mm(T.ps1[:, 0:16], V("m4"), V("sel"), False, False)
+    wp("hh")
+    mm(T.ps1[:, 0:16], V("hh"), V("selm"), False, True)
+    mm(T.ps1[:, 16:32], V("c2"), V("sel"), True, False)
+    inc(mm(T.ps1[:, 16:32], V("hh"), V("sel"), False, True), "p_l3")
+    wa("p_ol")
+    inc(s_.activation(V("pay"), T.ps7[:, 0:64], F.Identity), "pay")
     wv("eci")
     inc(ts(V("ecl"), V("eci"), 0.0, 129.0, A.max, A.min), "ecl")
-    wv("p_ol")
-    inc(v.tensor_copy(V("pay"), T.ps7[:, 0:64]), "pay")
     wv("p_eb")
     inc(ts(V("mk"), T.ps6[:, 0:192], col(1), None, A.is_equal), "mk")
-    wv("p_l3")
-    inc(v.tensor_copy(V("l3"), T.ps1[:, 0:32]), "l3")
     wv("ecl", "win", "mk", "win0")
     inc(tt(V("yy"), T.win[:, 0:130].indirect(V("ecl")), V("mk"), A.mult), "yy")
-    inc(ts(V("zz"), V("fr"), col(3), None, A.is_equal), "k_z")
+    wv("p_l3")
+    inc(v.tensor_copy(V("l3"), T.ps1[:, 0:32]), "l3")
     ev = [0, 2, 4, 6, 8, 10, 12]
     od = [i for i in range(16) if i not in ev]
     wa("l3", "pay", "k_i")
@@ -255,14 +261,16 @@ def rank_program(g, core, T, topo):
         for d in range(2):
             inc(s_.activation(T.bb[:, 64 * i + 32 * d:64 * i + 32 * d + 32], V("ta", 32 * k, 32 * k + 32), F.Relu,
                               bias=V("pay", 16 * d + i, 16 * d + i + 1), scale=V("pay", 32 + 16 * d + i, 33 + 16 * d + i)), "c%d" % i)
-    for j in range(4):
-        inc(s_.activation(T[N("mark", f)][:, 512 * j:512 * j + 512], V("one"), F.Identity, bias=V("bgc", 0, 1), scale=0.0), N("mrk", f))
+    marks(h, range(2, 4))
+    marks(f, range(4))
+    for k in range(2):
+        inc(s_.activation(T[N("run", k)][:, 0:B0], V("one"), F.Identity, bias=V("bgc", 1, 2), scale=0.0), "rus")
     wp("yy", "k_z")
+    mm(T.ps4[:, 12:16], V("zz", 0, 128), V("yy", 0, 4), True, True)
     for b in range(16):
         x = mm(T.ps4[:, 0:12], V("zz", 15 - b, 143 - b), V("yy", b, 192, 16), b == 0, b == 15)
     inc(x, "p_pp")
     o = q * W
-    inc(v.tensor_copy(T.rx[:, o + 76:o + 80], V("fr", 0, 4)), "pad")
     wv("l3", "pay", "k_i")
     order = ev + od
     for n, i in enumerate(order):
@@ -273,17 +281,18 @@ def rank_program(g, core, T, topo):
                        V("pay", 16 * d + i, 16 * d + i + 1), A.is_equal, A.mult), "c%d" % i)
         if n == 10:
             wv("p_pp")
-            inc(v.tensor_copy(T.rx[:, o + 64:o + 76], T.ps4[:, 0:12]), "ptx")
+            inc(v.tensor_copy(T.rx[:, o + 64:o + 80], T.ps4[:, 0:16]), "ptx")
     for i in order:
         wp("c%d" % i)
         x = mm(T.ps2[:, 0:64], T.aa[:, 128 * i:128 * i + 128], T.bb[:, 64 * i:64 * i + 64], i == order[0], i == order[-1])
     inc(x, "p_x")
     wv("p_x")
     inc(v.tensor_copy(T.rx[:, o:o + 64], T.ps2[:, 0:64]), "tx")
-    to = [c for c in gates if c != core] + [cores[r] for r in near if r != q and cores[r] not in gates]
+    to = [c for c in gates if T.rank_of(c) is None] + [c for c in gates if c != core and T.rank_of(c) is not None]
+    to += [cores[r] for r in near if r != q and cores[r] not in gates]
     full = topo.mask(core, to[0])
     t = T.rx[:, o:o + W]
-    wt("g", g, "ptx", "pad", "tx")
+    wt("g", g, "ptx", "tx")
     g.remote_dma_fused([RemoteDMATransfer(srcs=[t], dsts=[t] * len(to), dst_ids=[did(c) for c in to], dma_engine_mask=full,
                                           remote_sem=S.nx)], local_sem=S.ls)
     g.sem_inc(S.go, 1)
@@ -312,31 +321,36 @@ def rank_program(g, core, T, topo):
     wv("bi")
     inc(ts(V("base0"), V("b0i"), 512.0, None, A.mult), "bs")
     inc(ts(V("base1"), V("b1i"), 4.0, 512.0, A.min, A.mult), "bs")
+    wv("bs")
+    for k in range(2):
+        inc(ts(V(N("bass", k)), V(N("base", k)), float(B0), None, A.add), "bss")
     wv("src0")
     inc(ts(V("src"), V("src"), 2.0, None, A.mult), "src")
     inc(ts(T.tw[:, 0:4], V("big"), -2.0, None, A.mult), "tws")
     for k in range(2):
-        inc(ts(T[N("run", k)][:, 0:4], V("big"), -2.0, None, A.mult), "rus")
+        inc(ts(T[N("run", k)][:, B0:B0 + 1], V("big", 0, 1), -2.0, None, A.mult), "rus")
     inc(v.tensor_copy(V("erf", r=1), T.erow[:]), "erf")
     inc(v.memset(V("onef", r=1), 1.0), "erf")
 
     psx = {h: T.ps0, f: T.ps1}
+    psx0 = {h: T.ps2[:, 0:32], f: T.ps2[:, 64:96]}
     psp = {h: T.ps3, f: T.ps4}
     psd = {h: T.ps5, f: T.ps6}
 
     def pe_base(k):
-        wp("k_s", "k_d", "bs")
+        wp("k_s", "k_d", "bs", "bss")
         bs = N("base", k)
-        mm(psp[k][:, 0:20], V("s_o"), V(bs), True, False)
+        mm(psp[k][:, 0:20], V("s_o"), V(N("bass", k)), True, False)
         mm(psd[k][:, 0:20], V("s_d"), V(bs), True, False)
         mm(psd[k][:, 1:20], V("s_b"), V(bs, 0, 19), False, False)
 
     def pe_lists(k):
         for j, s in enumerate(ranks[k]):
-            p = psx[k][:, 32 * j:32 * j + 32]
+            p = psx[k][:, 32 * j:32 * j + 32] if j else psx0[k]
             mm(p, V("s_o"), T.rx[:, s * W:s * W + 32], True, False)
             x = mm(p, V("s_o"), T.rx[:, s * W + 32:s * W + 64], False, True)
-        inc(x, N("p_xl", k))
+            if j in (0, 3):
+                inc(x, N("p_xl" if j else "p_x0", k))
 
     def pe_borders(k):
         P, D = psp[k], psd[k]
@@ -352,52 +366,51 @@ def rank_program(g, core, T, topo):
         inc(x2, N("p_p", k))
 
     def gather(k, j):
-        wa(N("xo", k), "ldt", "tws")
+        wa(N("xo" if j else "xp", k), "ldt", "tws")
         inc(s_.activation(T[N("gd", k)][:, 512 * j:512 * j + 512], T.tw[:].indirect(V(N("xo", k), 32 * j, 32 * j + 32)), F.Copy),
             N("g" + "abcd"[j], k))
 
     def offsets(k):
+        wv(N("p_x0", k))
+        inc(v.tensor_copy(V(N("xo", k), 0, 32), psx0[k]), N("xp", k))
         wv(N("p_xl", k))
-        inc(v.tensor_copy(V(N("xo", k)), psx[k][:, 0:128]), N("xo", k))
+        inc(v.tensor_copy(V(N("xo", k), 32, 128), psx[k][:, 32:128]), N("xo", k))
 
     def borders(k):
         def n(x):
             return V(N(x, k))
         wv(N("p_p", k), "iom")
-        inc(ts(n("nd"), psd[k][:, 0:20], 0.0, None, A.is_gt), N("nd", k))
-        inc(tt(n("pt"), psp[k][:, 0:20], V("trash"), A.subtract), N("pt", k))
-        wv(N("nd", k), N("pt", k))
-        inc(tt(n("sa"), n("nd"), n("pt"), A.mult), N("sa", k))
-        inc(tt(n("pk"), psp[k][:, 0:20], n("nd"), A.mult), N("pk", k))
+        inc(ts(n("dk"), psd[k][:, 0:20], 0.0, -4096.0, A.is_le, A.mult), N("dk", k))
+        wv(N("dk", k))
+        inc(tt(n("sa"), psp[k][:, 0:20], n("dk"), A.add), N("sa", k))
         wv(N("sa", k))
-        inc(tt(n("sb"), n("sa"), V("trash"), A.add), N("sb", k))
-        wv(N("pk", k))
-        inc(v.tensor_copy(n("po"), n("pk")), N("po", k))
+        inc(tt(n("sb"), n("sa"), V("trash"), A.max), N("sb", k))
         wv(N("sb", k))
         inc(v.tensor_copy(n("sc"), n("sb")), N("sc", k))
         wv(N("sc", k), "src", N("mrk", k))
-        inc(v.tensor_copy(T[N("mark", k)][:].indirect(n("sc")), V("src")), N("sct", k))
+        inc(v.tensor_copy(T[N("mark", k)][:, 0:B0 + HB + 1].indirect(n("sc")), V("src")), N("sct", k))
 
-    def scans(k, js):
+    def scan(k, a, b):
         run = T[N("run", k)]
-        wv(N("sct", k), "rus")
-        for j in js:
-            wv(N("g" + "abcd"[j], k))
-            if j:
-                wv(N("r" + "abcd"[j - 1], k))
-            inc(v.tensor_tensor_scan(run[:, 4 + 512 * j:516 + 512 * j], T[N("mark", k)][:, 512 * j:512 * j + 512],
-                                     T[N("gd", k)][:, 512 * j:512 * j + 512], run[:, 3 + 512 * j:4 + 512 * j], A.min, A.max),
-                N("r" + "abcd"[j], k))
+        x, y = 512 * a, 512 * b
+        wv(N("sct", k), "rus", *[N("g" + c, k) for c in "abcd"[a:b]])
+        wv(*[N("r" + c, k) for c in "abcd"[max(a - 1, 0):a]])
+        inc(v.tensor_tensor_scan(run[:, B0 + 1 + x:B0 + 1 + y], T[N("mark", k)][:, B0 + x:B0 + y], T[N("gd", k)][:, x:y],
+                                 run[:, B0 + x:B0 + x + 1], A.min, A.max), N("r" + "abcd"[b - 1], k))
 
-    def pick(k, both):
-        o, n = ((12, 8) if both else (0, 12)) if k == 0 else ((0, 8) if both else (8, 12))
-        wt("v" if both else "a", v if both else s_, N("po", k), "rus", *[N("r" + c, k) for c in "abcd"])
-        out = T[N("pick", k)][:, 16 * o:16 * (o + n)]
-        i = T[N("run", k)][:, 3:HB + 4].indirect(V(N("po", k), o, o + n))
-        inc(v.tensor_copy(out, i) if both else s_.activation(out, i, F.Copy), N("pib" if both else "pik", k))
+    def pick(k, a, b, eng, sem, n=4):
+        o, e = 4 * (a - 3 * k), 4 * (b + 1 - 3 * k)
+        wt("v" if eng is v else "a", eng, N("sc", k), "rus", N("r" + "abcd"[n - 1], k))
+        out = T[N("pick", k)][:, 16 * o:16 * e]
+        i = T[N("run", k)][:, 0:B0 + 512 * n + 1].indirect(V(N("sc", k), o, e))
+        inc(v.tensor_copy(out, i) if eng is v else s_.activation(out, i, F.Copy), sem)
 
     def piece(d):
         return T.pick0[:, 64 * d:64 * (d + 1)] if d < 4 else T.pick1[:, 64 * (d - 3):64 * (d - 2)]
+
+    def join(d, sem, *need):
+        wv(*need)
+        inc(tt(piece(d), T.pick0[:, 64 * d:64 * d + 64], T.pick1[:, 64 * (d - 3):64 * (d - 2)], A.max), sem)
 
     pe_base(h)
     pe_base(f)
@@ -414,37 +427,54 @@ def rank_program(g, core, T, topo):
     for j in range(4):
         gather(h, j)
     borders(h)
-    wp("fx")
+    wp("fx", N("xp", h))
     pe_lists(f)
     pe_borders(f)
-    scans(h, range(3))
+    scan(h, 0, 1)
+    scan(h, 1, 2)
+    scan(h, 2, 3)
     offsets(f)
-    scans(h, range(3, 4))
-    pick(h, True)
     for j in range(4):
         gather(f, j)
+    scan(h, 3, 4)
     borders(f)
-    scans(f, range(4))
-    pick(f, True)
-    pick(f, False)
-    pick(h, False)
+    scan(f, 0, 2)
+    scan(f, 2, 3)
     fb, nb = (4, 3) if h == 0 else (3, 4)
-    wv("pib0", "pib1")
-    for d, sem in ((fb, "cmf"), (nb, "cmn")):
-        a, b = T.pick0[:, 64 * d:64 * d + 64], T.pick1[:, 64 * (d - 3):64 * (d - 2)]
-        inc(tt(piece(d), a, b, A.max), sem)
+    if h == 0:
+        pick(f, fb, fb, v, "pf", 3)
+        pick(f, 5, 5, s_, "pe", 3)
+        pick(h, 3, 4, s_, N("pib", h))
+        scan(f, 3, 4)
+        join(fb, "cmf", "pf", N("pib", h))
+        pick(f, 6, 7, s_, "pl")
+        need = (("cmf", "pe"), ("pl",))
+    else:
+        pick(f, 0, 1, s_, "pe", 3)
+        pick(h, 3, 4, s_, N("pib", h))
+        scan(f, 3, 4)
+        pick(f, fb, fb, v, "pf")
+        pick(f, 2, 2, s_, "pl")
+        join(fb, "cmf", "pf", N("pib", h))
+        need = (("pe",), ("pl", "cmf"))
+    pick(f, nb, nb, v, "pn")
+    join(nb, "cmn", "pn")
+    pick(h, near[0] if h == 0 else 5, 2 if h == 0 else near[-1], s_, N("pik", h))
+    ms = split(full, 2)
+    for e in range(2):
+        wt("g", g, *need[e])
+        tr = [RemoteDMATransfer(srcs=[piece(far[k])], dsts=[T.gl[:, 64 * me:64 * me + 64]], dst_ids=[did(gates[k])],
+                                dma_engine_mask=ms[k % 2], remote_sem=S.gx) for k in (2 * e, 2 * e + 1) if gates[k] != core]
+        g.remote_dma_fused(tr, local_sem=S.ls)
+        nls += 8 * len(tr)
     ms = split(full, 4)
-    wt("g", g, "cmf", N("pik", f))
-    tr = [RemoteDMATransfer(srcs=[piece(far[k])], dsts=[T.gl[:, 64 * me:64 * me + 64]], dst_ids=[did(c)], dma_engine_mask=ms[k],
-                            remote_sem=S.gx) for k, c in enumerate(gates) if c != core]
-    g.remote_dma_fused(tr, local_sem=S.ls)
     wt("g", g, "cmn", N("pik", h))
     g.remote_dma_fused([RemoteDMATransfer(srcs=[piece(r)], dsts=[T.nl[:, 64 * me:64 * me + 64]], dst_ids=[did(cores[r])],
                                           dma_engine_mask=ms[3 - k], remote_sem=S.ne2) for k, r in enumerate([r for r in near if r != q])],
                        local_sem=S.ls)
-    nls += 4 * len(tr) + 4 * n3
+    nls += 4 * n3
     if gate:
-        g.wait_ge(S.gx, 4 * n3)
+        g.wait_ge(S.gx, 8 * n3)
         fold([piece(fd) if r == q else T.gl[:, 64 * k:64 * k + 64] for k, r in enumerate(near)])
         nls += 8
     b0 = 0

@@ -1,16 +1,21 @@
 from concourse.bass import DstId, RemoteDMATransfer
 from concourse.mybir import dt, AluOpType, AxisListType, ActivationFunctionType
 
-W = 80
+W = 64
+WB = 32
 HB = 2048
 B0 = 512
-CUT = (0, 6656, 8192)
+BIG = 4096
+CUT = (0, 5888, 8192)
 
 SCRATCH = {
     "v": ("sbuf", [128, 128], "int32"), "endw": ("sbuf", [16, 32], "int32"), "erow": ("sbuf", [1, 192], "int32"),
     "aa": ("sbuf", [128, 2048], "bfloat16"), "bb": ("sbuf", [128, 1024], "bfloat16"), "win": ("sbuf", [128, 132], "float32"),
-    "rx": ("sbuf", [128, 8 * W], "float16"), "tw": ("sbuf", [128, 8196], "float32"),
-    "nl": ("sbuf", [128, 256], "float32"), "gl": ("sbuf", [128, 256], "float32"), "fl": ("sbuf", [128, 64], "float32"),
+    "rx": ("sbuf", [128, 8 * W], "float16"), "bx": ("sbuf", [128, 8 * WB], "float16"), "tw": ("sbuf", [128, 8196], "float32"),
+    "fo": ("sbuf", [128, 128], "uint16"), "fc": ("sbuf", [128, 24], "uint16"),
+    "fs": ("sbuf", [128, 256], "uint16"), "cs": ("sbuf", [128, 48], "uint16"),
+    "nl": ("sbuf", [128, 256], "float32"), "gl": ("sbuf", [128, 512], "float32"), "gm": ("sbuf", [128, 384], "float32"),
+    "fl": ("sbuf", [128, 64], "float32"),
 }
 for _h in range(2):
     for _n, _w, _d in (("mark", B0 + HB + 16, "bfloat16"), ("gd", HB, "float32"), ("run", B0 + HB + 4, "float32"), ("pick", 320, "float32")):
@@ -19,13 +24,13 @@ for _b in range(8):
     SCRATCH["ps%d" % _b] = ("psum", [128, 512], "float32")
 LAY = {}
 for _a, _d, _l in (
-    ("ai", "int32", "pi 4 ri 4 ii 4 fr 144 frr 128 fri 128 part 128 oli 128 ohi 128 eri 192 eci 12 bq 32 b0i 20 b1i 20"),
+    ("ai", "int32", "pi 4 ri 4 ii 4 fr 144 frr 128 fri 128 part 128 oli 128 ohi 128 eri 192 eci 12 bq 32 b0i 20"),
     ("ah", "float16", "c2 128 sel 16 selm 16 seln 16 zz 144 m4 128 hh 128 ol 128 oh 128 mk 192 yy 192 "
-                      "s_o 128 s_a 128 s_d 128 s_b 128 base0 20 base1 20 bass0 20 bass1 20"),
+                      "s_o 128 s_a 128 s_d 128 s_b 128"),
     ("af", "float32", "cf 8 rep 128 onef 128 big 4 bgc 4 l3 32 pay 64 endf 32 erf 192 trash 20 eb 80 ne 64 ze 64 zf 64 "
                       "ya 64 yb 64 yc 64 yd 64 ye 64 dk0 20 dk1 20 sa0 20 sa1 20 sb0 20 sb1 20"),
     ("ab", "bfloat16", "selr 16 iob 128 bo 128 nbo 128 nt 128 o4 128 ic 128 erh 192 erq 192 ta 512 src 320 one 512"),
-    ("au", "uint16", "xo0 128 xo1 128 sc0 20 sc1 20 ecl 12"),
+    ("au", "uint16", "xo0 128 sc0 20 ecl 12"),
 ):
     _o = 0
     _p = _l.split()
@@ -34,12 +39,12 @@ for _a, _d, _l in (
         _o += int(_p[_k + 1])
     SCRATCH[_a] = ("sbuf", [128, _o], _d)
 
-SEMAPHORES = ["ldi", "lde", "ldr", "ldt", "st", "nx", "fx", "ls", "ne2", "gx", "ff", "go",
+SEMAPHORES = ["ldi", "lde", "ldr", "ldt", "st", "nx", "nb", "fx", "fy", "ls", "ne2", "gx0", "gx1", "hm", "hn", "ff", "go",
               "io", "io1", "iom", "k_ri", "k_cf", "k_cg", "k_fr", "k_b", "k_c", "k_z", "k_i", "k_n", "k_t", "bg0", "bg", "tws", "rus",
               "endf", "eri", "erh", "erq", "p_e", "eci", "ecl", "p_eb", "mk", "part", "o4", "ic", "s4", "s4b", "win0", "win",
               "m4", "hh", "oli", "olh", "p_ol", "pay", "p_l3", "l3", "ta", "yy", "p_pp", "p_x", "ptx", "tx",
-              "k_s", "k_d", "bq", "bi", "bs", "bss", "src0", "src", "erf", "p_z", "ebz", "eb", "ne", "ze", "zf", "mrk0", "mrk1",
-              "cmf", "cmn", "pe", "pl", "pf", "pn", "ya", "yb", "yc", "yd", "ye"] + ["c%d" % i for i in range(16)]
+              "k_s", "k_d", "bq", "bi", "src0", "src", "erf", "p_z", "ebz", "eb", "ne", "ze", "zf", "mrk0", "mrk1",
+              "cmf", "cmn", "rus0", "rx", "pfn", "pe", "pl", "pf", "pn", "ya", "yb", "yc", "yd", "ye"] + ["c%d" % i for i in range(16)]
 for _h in range(2):
     SEMAPHORES += ["%s%d" % (n, _h) for n in ("p_xl", "p_p", "p_x0", "xp", "xo", "dk", "sa", "sb", "sc", "sct",
                                                "ga", "gb", "gc", "gd", "ra", "rb", "rc", "rd", "pik", "pib")]
@@ -64,40 +69,21 @@ def rank_program(g, core, T, topo):
     h = chips.index(topo.chip(core))
     f = 1 - h
     near, far = ranks[h], ranks[f]
-    gates = [c for c in range(64) if topo.chip(c) == chips[h] and all(topo.may_write(c, cores[d]) for d in far)][:len(far)]
-    gate = core in gates
-    if q is None and not gate:
+    gates = [c for c in range(64) if topo.chip(c) == chips[h] and T.rank_of(c) is None and all(topo.may_write(c, cores[d]) for d in far)]
+    gates = [[c for c in gates if topo.die(c) == d][0] for d in range(2)]
+    if q is None and core not in gates:
         return
     S = T.sem
-    fd = far[gates.index(core)] if gate else None
     n3 = len(near) - (0 if q is None else 1)
 
     def did(c):
         a = topo.addr(c)
         return DstId(rid=a[0], pnc=a[1])
 
-    def pass_on():
-        t = T.rx[:, near[0] * W:(near[-1] + 1) * W]
-        a = topo.addr(cores[fd])
-        g.remote_dma(t, t, S.fx, S.ls, a[1], a[0], topo.mask(core, cores[fd]))
-
-    def fold(srcs):
-        g.remote_dma_fused([RemoteDMATransfer(srcs=srcs, dsts=[T.fl[:]], dst_ids=[did(cores[fd])], alu_op=2,
-                                              dma_engine_mask=topo.mask(core, cores[fd]), remote_sem=S.ff)], local_sem=S.ls)
-
-    if q is None:
-        g.wait_ge(S.nx, 16 * n3)
-        pass_on()
-        g.wait_ge(S.gx, 8 * n3)
-        fold([T.gl[:, 64 * k:64 * k + 64] for k in range(len(near))])
-        g.wait_ge(S.ls, 16)
-        return
-
-    me = near.index(q)
     A = AluOpType
     F = ActivationFunctionType
     v, s_, pe, sy = g.vector, g.scalar, g.tensor, g.sync
-    cnt = {}
+    cnt = {"nx": 16 * n3, "nb": 16 * n3}
     seen = {}
 
     def V(n, a=0, b=None, st=1, r=128):
@@ -131,8 +117,120 @@ def rank_program(g, core, T, topo):
     def N(n, k):
         return "%s%d" % (n, k)
 
+    def col(k, n=128):
+        return V("cf", k, k + 1, r=n)
+
     mm = pe.matmul
     ts, tt = v.tensor_scalar, v.tensor_tensor
+    ri, ii, fr = V("ri", 0, 1), V("ii", 0, 1), V("fr", 0, 128)
+
+    def rows():
+        wv("io")
+        inc(ts(ri, V("pi", 0, 1), 4, None, A.arith_shift_right), "k_ri")
+        inc(ts(ii, V("pi", 0, 1), 15, None, A.bitwise_and), "k_ri")
+        inc(ts(V("frr"), fr, 4, None, A.arith_shift_right), "k_fr")
+        inc(ts(V("fri"), fr, 15, None, A.bitwise_and), "k_fr")
+        wv("k_ri")
+
+    def pickers(d, so, sa, sb, sd, c):
+        inc(ts(col(c), ri, float(d), None, A.is_equal), "k_cg")
+        inc(ts(col(c + 1), ri, float(d), -1.0, A.is_equal, A.mult), "k_cg")
+        wv("k_cg", "k_fr", "k_cf")
+        inc(ts(V(so), V("fri"), col(1), col(c), A.is_equal, A.mult), "k_s")
+        inc(ts(V(sa), V("fri"), col(4), col(c), A.is_equal, A.mult), "k_s")
+        inc(ts(V(sb), V("fri"), col(5), col(c + 1), A.is_equal, A.mult), "k_d")
+        wv("k_s")
+        inc(tt(V(sd), V(so), V(sa), A.subtract), "k_d")
+
+    def pe_base(P, D, so, sd, sb, s):
+        o = s * WB + 12
+        mm(P[:, 0:20], V(so), T.bx[:, o:o + 20], True, False)
+        mm(D[:, 0:20], V(sd), T.bx[:, o:o + 20], True, False)
+        mm(D[:, 1:20], V(sb), T.bx[:, o:o + 19], False, False)
+
+    def pe_borders(P, D, so, sd, sb, e):
+        for s in near:
+            o = c0(s) - 12 * h
+            b = s * WB
+            w = min(12, 19 - o)
+            x1 = mm(P[:, o:o + 12], V(so), T.bx[:, b:b + 12], False, s == near[-1])
+            mm(D[:, o:o + 12], V(sd), T.bx[:, b:b + 12], False, False)
+            x2 = mm(D[:, o + 1:o + 1 + w], V(sb), T.bx[:, b:b + w], False, s == near[-1])
+        inc(x1, N("p_p", e))
+        inc(x2, N("p_p", e))
+
+    def pe_lists(p0, p, so, e):
+        for j, s in enumerate(near):
+            x = p[:, 32 * j:32 * j + 32] if j else p0
+            mm(x, V(so), T.rx[:, s * W:s * W + 32], True, False)
+            y = mm(x, V(so), T.rx[:, s * W + 32:s * W + 64], False, True)
+            if j in (0, 3):
+                inc(y, N("p_xl" if j else "p_x0", e))
+
+    def places(P, D, e, out):
+        def n(x):
+            return V(N(x, e))
+        wv(N("p_p", e), "iom")
+        inc(ts(n("dk"), D[:, 0:20], 0.0, float(BIG), A.is_gt, A.mult), N("dk", e))
+        wv(N("dk", e))
+        inc(tt(n("sa"), P[:, 0:20], n("dk"), A.add), N("sa", e))
+        wv(N("sa", e))
+        inc(tt(n("sb"), n("sa"), V("trash"), A.max), N("sb", e))
+        wv(N("sb", e))
+        inc(ts(out, n("sb"), float(B0 - BIG), None, A.add), N("sc", e))
+
+    inc(g.iota(V("pi", 0, 1), [[1, 1]], 0, 1), "io")
+    inc(g.iota(V("fr"), [[1, 144]], 0, 0), "io")
+
+    def trash():
+        inc(g.iota(V("trash"), [[16, 20]], BIG - B0, 1, allow_small_or_imprecise_dtypes=True), "iom")
+
+    if q is None:
+        mine = far[gates.index(core)::2]
+        m = topo.mask(core, cores[mine[0]])
+
+        def send(out, src, e, sem):
+            a = topo.addr(cores[mine[e]])
+            g.remote_dma(out, src, sem, S.ls, a[1], a[0], m)
+
+        trash()
+        rows()
+        inc(v.tensor_copy(col(1), ii), "k_cf")
+        inc(ts(col(4), ii, 1.0, None, A.add), "k_cf")
+        inc(ts(col(5), ii, -15.0, None, A.add), "k_cf")
+        fac = (("s_o", "s_a", "s_b", "s_d"), ("ol", "oh", "m4", "hh"))
+        for e in range(2):
+            inc(v.memset(T.cs[:, 24 * e + 20:24 * e + 24], 0), N("xp", e))
+            pickers(mine[e], *fac[e], (2, 6)[e])
+        wp("k_s", "k_d", "nb")
+        for e in range(2):
+            so, sa, sb, sd = fac[e]
+            P, D = (T.ps1, T.ps2) if e == 0 else (T.ps4, T.ps5)
+            pe_base(P, D, so, sd, sb, near[0])
+            pe_borders(P, D, so, sd, sb, e)
+            places(P, D, e, T.cs[:, 24 * e:24 * e + 20])
+            wt("g", g, N("xp", e), N("sc", e))
+            send(T.fc[:], T.cs[:, 24 * e:24 * e + 24], e, S.fy)
+        wp("nx")
+        for e in range(2):
+            X = T.ps0 if e == 0 else T.ps3
+            pe_lists(X[:, 0:32], X, fac[e][0], e)
+            wv(N("p_x0", e), N("p_xl", e))
+            inc(v.tensor_copy(T.fs[:, 128 * e:128 * e + 128], X[:, 0:128]), N("xo", e))
+            wt("g", g, N("xo", e))
+            send(T.fo[:], T.fs[:, 128 * e:128 * e + 128], e, S.fx)
+        for e in range(2):
+            gl, gm = 256 * e, 192 * e
+            v.wait_ge(S["gx%d" % e], 8 * n3)
+            v.tensor_tensor(T.gm[:, gm:gm + 128], T.gl[:, gl:gl + 128], T.gl[:, gl + 128:gl + 256], A.max).then_inc(S.hm, 1)
+            v.wait_ge(S.hm, e + 1)
+            v.tensor_tensor(T.gm[:, gm + 128:gm + 192], T.gm[:, gm:gm + 64], T.gm[:, gm + 64:gm + 128], A.max).then_inc(S.hn, 1)
+            g.wait_ge(S.hn, e + 1)
+            send(T.fl[:], T.gm[:, gm + 128:gm + 192], e, S.ff)
+        g.wait_ge(S.ls, 48)
+        return
+
+    me = near.index(q)
     sy.dma_start(T.endw[:], T.end[:]).then_inc(S.lde, 16)
     s_.dma_start(T.erow[:], T.end[:, c0(q):c0(q) + 12]).then_inc(S.ldr, 16)
     for k in range(8):
@@ -142,29 +240,17 @@ def rank_program(g, core, T, topo):
         sy.dma_start(T.tw[:, 4 + CUT[k]:4 + CUT[k + 1]], T.tab[:, CUT[k]:CUT[k + 1]]).then_inc(S.ldt, 16)
 
     load(0)
-    cnt.update({"lde": 16, "ldr": 16, "ldi": 128, "ldt": 32, "nx": 16 * n3, "fx": 8, "ff": 8, "ne2": 4 * n3, "go": 1})
-    inc(g.iota(V("pi", 0, 1), [[1, 1]], 0, 1), "io")
-    inc(g.iota(V("fr"), [[1, 144]], 0, 0), "io")
+    cnt.update({"lde": 16, "ldr": 16, "ldi": 128, "ldt": 32, "fx": 8, "fy": 8, "ff": 8, "ne2": 4 * n3, "go": 1})
     inc(g.iota(V("one"), [[0, 512]], 1, 0, allow_small_or_imprecise_dtypes=True), "io1")
     inc(g.iota(V("iob"), [[1, 128]], 0, 0, allow_small_or_imprecise_dtypes=True), "k_i")
-    inc(g.iota(V("trash"), [[16, 20]], 0, 1, allow_small_or_imprecise_dtypes=True), "iom")
+    trash()
     inc(v.memset(V("big"), 2.0 ** 99), "bg0")
     inc(v.memset(T.win[:, 0:1], 0.0), "win0")
     inc(v.memset(T.win[:, 129:130], 0.0), "win0")
     wv("bg0")
     inc(ts(V("bgc", 0, 1), V("big", 0, 1), 4.0, None, A.mult), "bg")
     inc(ts(V("bgc", 1, 2), V("big", 0, 1), -2.0, None, A.mult), "bg")
-    wv("io")
-    ri, ii, fr = V("ri", 0, 1), V("ii", 0, 1), V("fr", 0, 128)
-    inc(ts(ri, V("pi", 0, 1), 4, None, A.arith_shift_right), "k_ri")
-    inc(ts(ii, V("pi", 0, 1), 15, None, A.bitwise_and), "k_ri")
-    inc(ts(V("frr"), fr, 4, None, A.arith_shift_right), "k_fr")
-    inc(ts(V("fri"), fr, 15, None, A.bitwise_and), "k_fr")
-    wv("k_ri")
-
-    def col(k, n=128):
-        return V("cf", k, k + 1, r=n)
-
+    rows()
     inc(v.tensor_copy(col(0), ri), "k_cf")
     inc(v.tensor_copy(col(1), ii), "k_cf")
     inc(ts(col(2), ri, 16.0, None, A.mult), "k_cf")
@@ -182,6 +268,8 @@ def rank_program(g, core, T, topo):
     inc(ts(V("zz"), V("fr"), col(3), None, A.is_equal), "k_z")
     wt("g", g, "k_n")
     inc(g.affine_select(V("nt"), V("nbo"), [[-1, 128]], A.is_ge, 0.0, 0, 1), "k_t")
+    if h == 0:
+        inc(g.iota(T.run0[:, B0 + 1:B0 + 1537], [[0, 1536]], 0, 0, allow_small_or_imprecise_dtypes=True), "rus0")
 
     def marks(k, js):
         wa("bg", "io1")
@@ -231,6 +319,7 @@ def rank_program(g, core, T, topo):
     inc(tt(V("m4"), T.ps0[:, 0:128], V("o4"), A.mult), "m4")
     wv("p_e")
     inc(ts(V("eci"), T.ps5[:, c0(q):c0(q) + 12], 8.5 - 2048.0 * q, 1.0 / 16, A.add, A.mult), "eci")
+    inc(ts(V("bq"), T.ps5[:, 0:32], -1023.5, 1.0 / 2048, A.add, A.mult), "bq")
     wv("m4")
     inc(ts(V("hh"), V("m4"), 1.0 / 16, 1535.53125, A.mult, A.add), "hh")
     wa("s4b", "win0")
@@ -249,6 +338,11 @@ def rank_program(g, core, T, topo):
     inc(ts(V("mk"), T.ps6[:, 0:192], col(1), None, A.is_equal), "mk")
     wv("ecl", "win", "mk", "win0")
     inc(tt(V("yy"), T.win[:, 0:130].indirect(V("ecl")), V("mk"), A.mult), "yy")
+    wv("bq")
+    if h == 0:
+        inc(ts(V("b0i"), V("bq", 0, 20), 0.0, 4.0, A.max, A.min), "bi")
+    else:
+        inc(ts(V("b0i"), V("bq", 12, 32), -4.0, 0.0, A.add, A.max), "bi")
     wv("p_l3")
     inc(v.tensor_copy(V("l3"), T.ps1[:, 0:32]), "l3")
     ev = [0, 2, 4, 6, 8, 10, 12]
@@ -266,11 +360,10 @@ def rank_program(g, core, T, topo):
     for k in range(2):
         inc(s_.activation(T[N("run", k)][:, 0:B0], V("one"), F.Identity, bias=V("bgc", 1, 2), scale=0.0), "rus")
     wp("yy", "k_z")
-    mm(T.ps4[:, 12:16], V("zz", 0, 128), V("yy", 0, 4), True, True)
     for b in range(16):
         x = mm(T.ps4[:, 0:12], V("zz", 15 - b, 143 - b), V("yy", b, 192, 16), b == 0, b == 15)
     inc(x, "p_pp")
-    o = q * W
+    o, ob = q * W, q * WB
     wv("l3", "pay", "k_i")
     order = ev + od
     for n, i in enumerate(order):
@@ -279,51 +372,35 @@ def rank_program(g, core, T, topo):
             for d in range(2):
                 inc(ts(T.bb[:, 64 * i + 32 * d:64 * i + 32 * d + 32], V("iob", 0, 32), V("l3", 16 + i, 17 + i),
                        V("pay", 16 * d + i, 16 * d + i + 1), A.is_equal, A.mult), "c%d" % i)
-        if n == 10:
-            wv("p_pp")
-            inc(v.tensor_copy(T.rx[:, o + 64:o + 80], T.ps4[:, 0:16]), "ptx")
+        if n == 4:
+            wv("p_pp", "bi")
+            inc(v.tensor_copy(T.bx[:, ob:ob + 12], T.ps4[:, 0:12]), "ptx")
+            inc(ts(T.bx[:, ob + 12:ob + 32], V("b0i"), 4.0, 512.0, A.min, A.mult), "ptx")
     for i in order:
         wp("c%d" % i)
         x = mm(T.ps2[:, 0:64], T.aa[:, 128 * i:128 * i + 128], T.bb[:, 64 * i:64 * i + 64], i == order[0], i == order[-1])
     inc(x, "p_x")
     wv("p_x")
     inc(v.tensor_copy(T.rx[:, o:o + 64], T.ps2[:, 0:64]), "tx")
-    to = [c for c in gates if T.rank_of(c) is None] + [c for c in gates if c != core and T.rank_of(c) is not None]
-    to += [cores[r] for r in near if r != q and cores[r] not in gates]
+    to = gates + [cores[r] for r in near if r != q]
     full = topo.mask(core, to[0])
-    t = T.rx[:, o:o + W]
-    wt("g", g, "ptx", "tx")
-    g.remote_dma_fused([RemoteDMATransfer(srcs=[t], dsts=[t] * len(to), dst_ids=[did(c) for c in to], dma_engine_mask=full,
-                                          remote_sem=S.nx)], local_sem=S.ls)
+
+    def tell(t, sem):
+        g.remote_dma_fused([RemoteDMATransfer(srcs=[t], dsts=[t] * len(to), dst_ids=[did(c) for c in to], dma_engine_mask=full,
+                                              remote_sem=sem)], local_sem=S.ls)
+
+    wt("g", g, "ptx")
+    tell(T.bx[:, ob:ob + WB], S.nb)
+    wt("g", g, "tx")
+    tell(T.rx[:, o:o + W], S.nx)
     g.sem_inc(S.go, 1)
     wt("sy", sy, "go")
     load(1)
-    nls = 16
-    if gate:
-        wt("g", g, "nx")
-        pass_on()
-        nls += 8
+    nls = 32
     inc(ts(col(4), ii, 1.0, None, A.add), "k_cg")
     inc(ts(col(5), ii, -15.0, None, A.add), "k_cg")
-    inc(ts(col(6), ri, float(q), None, A.is_equal), "k_cg")
-    inc(ts(col(7), ri, float(q), -1.0, A.is_equal, A.mult), "k_cg")
-    inc(ts(V("bq"), T.ps5[:, 0:32], -1023.5, 1.0 / 2048, A.add, A.mult), "bq")
     inc(v.memset(V("src"), -2.0 ** 99), "src0")
-    wv("k_cg")
-    inc(ts(V("s_o"), V("fri"), col(1), col(6), A.is_equal, A.mult), "k_s")
-    inc(ts(V("s_a"), V("fri"), col(4), col(6), A.is_equal, A.mult), "k_s")
-    inc(ts(V("s_b"), V("fri"), col(5), col(7), A.is_equal, A.mult), "k_d")
-    wv("bq")
-    inc(ts(V("b0i"), V("bq", 0, 20), 0.0, 4.0, A.max, A.min), "bi")
-    inc(ts(V("b1i"), V("bq", 12, 32), -4.0, 0.0, A.add, A.max), "bi")
-    wv("k_s")
-    inc(tt(V("s_d"), V("s_o"), V("s_a"), A.subtract), "k_d")
-    wv("bi")
-    inc(ts(V("base0"), V("b0i"), 512.0, None, A.mult), "bs")
-    inc(ts(V("base1"), V("b1i"), 4.0, 512.0, A.min, A.mult), "bs")
-    wv("bs")
-    for k in range(2):
-        inc(ts(V(N("bass", k)), V(N("base", k)), float(B0), None, A.add), "bss")
+    pickers(q, "s_o", "s_a", "s_b", "s_d", 6)
     wv("src0")
     inc(ts(V("src"), V("src"), 2.0, None, A.mult), "src")
     inc(ts(T.tw[:, 0:4], V("big"), -2.0, None, A.mult), "tws")
@@ -332,63 +409,30 @@ def rank_program(g, core, T, topo):
     inc(v.tensor_copy(V("erf", r=1), T.erow[:]), "erf")
     inc(v.memset(V("onef", r=1), 1.0), "erf")
 
-    psx = {h: T.ps0, f: T.ps1}
-    psx0 = {h: T.ps2[:, 0:32], f: T.ps2[:, 64:96]}
-    psp = {h: T.ps3, f: T.ps4}
-    psd = {h: T.ps5, f: T.ps6}
+    def XO(a, b, k):
+        return T.fo[:, a:b] if k == f else V("xo0", a, b)
 
-    def pe_base(k):
-        wp("k_s", "k_d", "bs", "bss")
-        bs = N("base", k)
-        mm(psp[k][:, 0:20], V("s_o"), V(N("bass", k)), True, False)
-        mm(psd[k][:, 0:20], V("s_d"), V(bs), True, False)
-        mm(psd[k][:, 1:20], V("s_b"), V(bs, 0, 19), False, False)
+    def SC(a, b, k):
+        return T.fc[:, a:b] if k == f else V("sc0", a, b)
 
-    def pe_lists(k):
-        for j, s in enumerate(ranks[k]):
-            p = psx[k][:, 32 * j:32 * j + 32] if j else psx0[k]
-            mm(p, V("s_o"), T.rx[:, s * W:s * W + 32], True, False)
-            x = mm(p, V("s_o"), T.rx[:, s * W + 32:s * W + 64], False, True)
-            if j in (0, 3):
-                inc(x, N("p_xl" if j else "p_x0", k))
+    def gather(k, j, eng=s_):
+        wt("v" if eng is v else "a", eng, "fx" if k == f else "xo0" if j else "xp0", "ldt", "tws")
+        out = T[N("gd", k)][:, 512 * j:512 * j + 512]
+        i = T.tw[:].indirect(XO(32 * j, 32 * j + 32, k))
+        inc(v.tensor_copy(out, i) if eng is v else s_.activation(out, i, F.Copy), N("g" + "abcd"[j], k))
 
-    def pe_borders(k):
-        P, D = psp[k], psd[k]
-        last = ranks[k][-1]
-        for s in ranks[k]:
-            o = c0(s) - 12 * k
-            b = s * W + 64
-            w = min(12, 19 - o)
-            x1 = mm(P[:, o:o + 12], V("s_o"), T.rx[:, b:b + 12], False, s == last)
-            mm(D[:, o:o + 12], V("s_d"), T.rx[:, b:b + 12], False, False)
-            x2 = mm(D[:, o + 1:o + 1 + w], V("s_b"), T.rx[:, b:b + w], False, s == last)
-        inc(x1, N("p_p", k))
-        inc(x2, N("p_p", k))
+    def scatter(k):
+        wv("fy" if k == f else "sc0", "src", N("mrk", k))
+        inc(v.tensor_copy(T[N("mark", k)][:, 0:B0 + HB + 1].indirect(SC(0, 20, k)), V("src")), N("sct", k))
 
-    def gather(k, j):
-        wa(N("xo" if j else "xp", k), "ldt", "tws")
-        inc(s_.activation(T[N("gd", k)][:, 512 * j:512 * j + 512], T.tw[:].indirect(V(N("xo", k), 32 * j, 32 * j + 32)), F.Copy),
-            N("g" + "abcd"[j], k))
-
-    def offsets(k):
-        wv(N("p_x0", k))
-        inc(v.tensor_copy(V(N("xo", k), 0, 32), psx0[k]), N("xp", k))
-        wv(N("p_xl", k))
-        inc(v.tensor_copy(V(N("xo", k), 32, 128), psx[k][:, 32:128]), N("xo", k))
-
-    def borders(k):
-        def n(x):
-            return V(N(x, k))
-        wv(N("p_p", k), "iom")
-        inc(ts(n("dk"), psd[k][:, 0:20], 0.0, -4096.0, A.is_le, A.mult), N("dk", k))
-        wv(N("dk", k))
-        inc(tt(n("sa"), psp[k][:, 0:20], n("dk"), A.add), N("sa", k))
-        wv(N("sa", k))
-        inc(tt(n("sb"), n("sa"), V("trash"), A.max), N("sb", k))
-        wv(N("sb", k))
-        inc(v.tensor_copy(n("sc"), n("sb")), N("sc", k))
-        wv(N("sc", k), "src", N("mrk", k))
-        inc(v.tensor_copy(T[N("mark", k)][:, 0:B0 + HB + 1].indirect(n("sc")), V("src")), N("sct", k))
+    def scan_first(j):
+        run = T[N("run", h)]
+        x = 512 * j
+        wv(N("sct", h), "rus", N("g" + "abcd"[j], h))
+        if j:
+            wv("rus0")
+        inc(v.tensor_tensor_scan(run[:, B0 + 1 + x:B0 + 513 + x], T[N("mark", h)][:, B0 + x:B0 + 512 + x], T[N("gd", h)][:, x:x + 512],
+                                 run[:, 0:1], A.min, A.max), "rx" if j else N("ra", h))
 
     def scan(k, a, b):
         run = T[N("run", k)]
@@ -398,11 +442,11 @@ def rank_program(g, core, T, topo):
         inc(v.tensor_tensor_scan(run[:, B0 + 1 + x:B0 + 1 + y], T[N("mark", k)][:, B0 + x:B0 + y], T[N("gd", k)][:, x:y],
                                  run[:, B0 + x:B0 + x + 1], A.min, A.max), N("r" + "abcd"[b - 1], k))
 
-    def pick(k, a, b, eng, sem, n=4):
+    def pick(k, a, b, eng, sem, n=4, after=None):
         o, e = 4 * (a - 3 * k), 4 * (b + 1 - 3 * k)
-        wt("v" if eng is v else "a", eng, N("sc", k), "rus", N("r" + "abcd"[n - 1], k))
+        wt("v" if eng is v else "a", eng, "fy" if k == f else "sc0", "rus", after if after else N("r" + "abcd"[n - 1], k))
         out = T[N("pick", k)][:, 16 * o:16 * e]
-        i = T[N("run", k)][:, 0:B0 + 512 * n + 1].indirect(V(N("sc", k), o, e))
+        i = T[N("run", k)][:, 0:B0 + 512 * n + 1].indirect(SC(o, e, k))
         inc(v.tensor_copy(out, i) if eng is v else s_.activation(out, i, F.Copy), sem)
 
     def piece(d):
@@ -412,71 +456,76 @@ def rank_program(g, core, T, topo):
         wv(*need)
         inc(tt(piece(d), T.pick0[:, 64 * d:64 * d + 64], T.pick1[:, 64 * (d - 3):64 * (d - 2)], A.max), sem)
 
-    pe_base(h)
-    pe_base(f)
+    fb, nb = (4, 3) if h == 0 else (3, 4)
+    j0 = 3 if h == 0 else 0
+    rest = [j for j in range(4) if j != j0]
+    P, D = T.ps3, T.ps5
+    wp("k_s", "k_d", "ptx")
+    pe_base(P, D, "s_o", "s_d", "s_b", q)
+    wp("nb")
+    pe_borders(P, D, "s_o", "s_d", "s_b", 0)
+    wp("nx", "tx")
+    pe_lists(T.ps2[:, 0:32], T.ps0, "s_o", 0)
+    places(P, D, 0, V("sc0"))
+    scatter(h)
+    wv("p_x00")
+    inc(v.tensor_copy(V("xo0", 0, 32), T.ps2[:, 0:32]), "xp0")
+    wv("p_xl0")
+    inc(v.tensor_copy(V("xo0", 32, 128), T.ps0[:, 32:128]), "xo0")
+    gather(h, j0)
+    gather(h, rest[0], v)
+    gather(h, rest[1])
     lo = 4 * q - 1 - c0(q)
     wp("erf")
     for k in range(5):
         if lo + k >= 0:
             x = mm(T.ps7[:, 16 * k:16 * k + 16], V("onef", r=1), V("erf", lo + k, 192, 12, 1), True, True)
     inc(x, "p_z")
-    wp("nx", "tx", "ptx")
-    pe_lists(h)
-    pe_borders(h)
-    offsets(h)
-    for j in range(4):
-        gather(h, j)
-    borders(h)
-    wp("fx", N("xp", h))
-    pe_lists(f)
-    pe_borders(f)
-    scan(h, 0, 1)
-    scan(h, 1, 2)
-    scan(h, 2, 3)
-    offsets(f)
-    for j in range(4):
+    scan_first(j0)
+    gather(f, 0)
+    pick(h, fb, fb, s_, "pfn", 4 if h == 0 else 1, "rx" if h == 0 else None)
+    for j in range(1, 4):
         gather(f, j)
-    scan(h, 3, 4)
-    borders(f)
+    scatter(f)
     scan(f, 0, 2)
     scan(f, 2, 3)
-    fb, nb = (4, 3) if h == 0 else (3, 4)
+    scan(f, 3, 4)
     if h == 0:
-        pick(f, fb, fb, v, "pf", 3)
-        pick(f, 5, 5, s_, "pe", 3)
-        pick(h, 3, 4, s_, N("pib", h))
-        scan(f, 3, 4)
-        join(fb, "cmf", "pf", N("pib", h))
+        pick(f, fb, 5, s_, "pf", 3)
         pick(f, 6, 7, s_, "pl")
-        need = (("cmf", "pe"), ("pl",))
+        need = (("cmf", "pf"), ("pl",))
     else:
         pick(f, 0, 1, s_, "pe", 3)
-        pick(h, 3, 4, s_, N("pib", h))
-        scan(f, 3, 4)
-        pick(f, fb, fb, v, "pf")
-        pick(f, 2, 2, s_, "pl")
-        join(fb, "cmf", "pf", N("pib", h))
-        need = (("pe",), ("pl", "cmf"))
-    pick(f, nb, nb, v, "pn")
-    join(nb, "cmn", "pn")
-    pick(h, near[0] if h == 0 else 5, 2 if h == 0 else near[-1], s_, N("pik", h))
+        pick(f, 2, fb, s_, "pf")
+        need = (("pe",), ("pf", "cmf"))
+    join(fb, "cmf", "pf", "pfn")
     ms = split(full, 2)
     for e in range(2):
         wt("g", g, *need[e])
-        tr = [RemoteDMATransfer(srcs=[piece(far[k])], dsts=[T.gl[:, 64 * me:64 * me + 64]], dst_ids=[did(gates[k])],
-                                dma_engine_mask=ms[k % 2], remote_sem=S.gx) for k in (2 * e, 2 * e + 1) if gates[k] != core]
-        g.remote_dma_fused(tr, local_sem=S.ls)
-        nls += 8 * len(tr)
+        g.remote_dma_fused([RemoteDMATransfer(srcs=[piece(far[2 * e + k])], dsts=[T.gl[:, 256 * e + 64 * me:256 * e + 64 * me + 64]],
+                                              dst_ids=[did(gates[k])], dma_engine_mask=ms[k], remote_sem=S["gx%d" % e]) for k in range(2)],
+                           local_sem=S.ls)
+        nls += 16
+    gather(h, rest[2])
+    if h == 0:
+        scan(h, 0, 1)
+        scan(h, 1, 2)
+        pick(f, nb, nb, v, "pn")
+        scan(h, 2, 4)
+    else:
+        scan(h, 1, 2)
+        scan(h, 2, 3)
+        pick(f, nb, nb, v, "pn")
+        scan(h, 3, 4)
+    pick(h, 2 if h == 0 else nb, nb if h == 0 else 5, v, N("pib", h))
+    pick(h, near[0] if h == 0 else 6, 1 if h == 0 else near[-1], s_, N("pik", h))
+    join(nb, "cmn", "pn", N("pib", h))
     ms = split(full, 4)
-    wt("g", g, "cmn", N("pik", h))
+    wt("g", g, "cmn", N("pib", h), N("pik", h))
     g.remote_dma_fused([RemoteDMATransfer(srcs=[piece(r)], dsts=[T.nl[:, 64 * me:64 * me + 64]], dst_ids=[did(cores[r])],
                                           dma_engine_mask=ms[3 - k], remote_sem=S.ne2) for k, r in enumerate([r for r in near if r != q])],
                        local_sem=S.ls)
     nls += 4 * n3
-    if gate:
-        g.wait_ge(S.gx, 8 * n3)
-        fold([piece(fd) if r == q else T.gl[:, 64 * k:64 * k + 64] for k, r in enumerate(near)])
-        nls += 8
     b0 = 0
     if lo < 0:
         inc(v.memset(V("eb", 0, 16), 0.0), "ebz")
@@ -492,16 +541,15 @@ def rank_program(g, core, T, topo):
     inc(ts(V("zf"), V("ze"), 2.0, None, A.mult), "zf")
     wv("cmn", N("pik", h), "zf")
     inc(tt(V("ya"), piece(q), V("zf"), A.max), "ya")
-    last = "ya"
+    nl = [T.nl[:, 64 * near.index(r):64 * near.index(r) + 64] for r in near if r != q]
     wv("ne2")
-    names = ["yb", "yc", "yd"]
-    for k, r in enumerate([r for r in near if r != q]):
-        wv(last)
-        j = near.index(r)
-        inc(tt(V(names[k]), V(last), T.nl[:, 64 * j:64 * j + 64], A.max), names[k])
-        last = names[k]
-    wv(last, "ff")
-    inc(tt(V("ye"), V(last), T.fl[:], A.max), "ye")
+    inc(tt(V("yb"), nl[0], nl[1], A.max), "yb")
+    wv("ya")
+    inc(tt(V("yc"), nl[2], V("ya"), A.max), "yc")
+    wv("yb", "yc")
+    inc(tt(V("yd"), V("yb"), V("yc"), A.max), "yd")
+    wv("yd", "ff")
+    inc(tt(V("ye"), V("yd"), T.fl[:], A.max), "ye")
     wt("sy", sy, "ye")
     sy.dma_start(T.y[:], V("ye")).then_inc(S.st, 16)
     sy.wait_ge(S.st, 16)

from concourse.bass import DstId, RemoteDMATransfer
from concourse.mybir import dt, AluOpType, AxisListType, ActivationFunctionType

W = 64
WB = 32
HB = 2048
B0 = 512
BIG = 4096
CUT = (0, 5888, 8192)

SCRATCH = {
    "v": ("sbuf", [128, 128], "int32"), "endw": ("sbuf", [16, 32], "int32"), "erow": ("sbuf", [1, 192], "int32"),
    "aa": ("sbuf", [128, 2048], "bfloat16"), "bb": ("sbuf", [128, 1024], "bfloat16"), "win": ("sbuf", [128, 132], "float32"),
    "rx": ("sbuf", [128, 8 * W], "float16"), "bx": ("sbuf", [128, 8 * WB], "float16"), "tw": ("sbuf", [128, 8196], "float32"),
    "fo": ("sbuf", [128, 128], "uint16"), "fc": ("sbuf", [128, 24], "uint16"),
    "fs": ("sbuf", [128, 256], "uint16"), "cs": ("sbuf", [128, 48], "uint16"),
    "nl": ("sbuf", [128, 256], "float32"), "gl": ("sbuf", [128, 512], "float32"), "gm": ("sbuf", [128, 384], "float32"),
    "fl": ("sbuf", [128, 64], "float32"),
}
for _h in range(2):
    for _n, _w, _d in (("mark", B0 + HB + 16, "bfloat16"), ("gd", HB, "float32"), ("run", B0 + HB + 4, "float32"), ("pick", 320, "float32")):
        SCRATCH["%s%d" % (_n, _h)] = ("sbuf", [128, _w], _d)
for _b in range(8):
    SCRATCH["ps%d" % _b] = ("psum", [128, 512], "float32")
LAY = {}
for _a, _d, _l in (
    ("ai", "int32", "pi 4 ri 4 ii 4 fr 144 frr 128 fri 128 part 128 oli 128 ohi 128 eri 192 eci 12 bq 32 b0i 20"),
    ("ah", "float16", "c2 128 sel 16 selm 16 seln 16 zz 144 m4 128 hh 128 ol 128 oh 128 mk 192 yy 192 "
                      "s_o 128 s_a 128 s_d 128 s_b 128"),
    ("af", "float32", "cf 8 rep 128 onef 128 big 4 bgc 4 l3 32 pay 64 endf 32 erf 192 trash 20 eb 80 ne 64 ze 64 zf 64 "
                      "ya 64 yb 64 yc 64 yd 64 ye 64 dk0 20 dk1 20 sa0 20 sa1 20 sb0 20 sb1 20"),
    ("ab", "bfloat16", "selr 16 iob 128 bo 128 nbo 128 nt 128 o4 128 ic 128 erh 192 erq 192 ta 512 src 320 one 512"),
    ("au", "uint16", "xo0 128 sc0 20 ecl 12"),
):
    _o = 0
    _p = _l.split()
    for _k in range(0, len(_p), 2):
        LAY[_p[_k]] = (_a, _o, int(_p[_k + 1]))
        _o += int(_p[_k + 1])
    SCRATCH[_a] = ("sbuf", [128, _o], _d)

SEMAPHORES = ["ldi", "lde", "ldr", "ldt", "st", "nx", "nb", "fx", "fy", "ls", "ne2", "gx0", "gx1", "hm", "hn", "ff", "go",
              "io", "io1", "iom", "k_ri", "k_cf", "k_cg", "k_fr", "k_b", "k_c", "k_z", "k_i", "k_n", "k_t", "bg0", "bg", "tws", "rus",
              "endf", "eri", "erh", "erq", "p_e", "eci", "ecl", "p_eb", "mk", "part", "o4", "ic", "s4", "s4b", "win0", "win",
              "m4", "hh", "oli", "olh", "p_ol", "pay", "p_l3", "l3", "ta", "yy", "p_pp", "p_x", "ptx", "tx",
              "k_s", "k_d", "bq", "bi", "src0", "src", "erf", "p_z", "ebz", "eb", "ne", "ze", "zf", "mrk0", "mrk1",
              "cmf", "cmn", "rus0", "rx", "pfn", "pe", "pl", "pf", "pn", "ya", "yb", "yc", "yd", "ye"] + ["c%d" % i for i in range(16)]
for _h in range(2):
    SEMAPHORES += ["%s%d" % (n, _h) for n in ("p_xl", "p_p", "p_x0", "xp", "xo", "dk", "sa", "sb", "sc", "sct",
                                               "ga", "gb", "gc", "gd", "ra", "rb", "rc", "rd", "pik", "pib")]


def split(mask, parts):
    bits = [b for b in range(mask.bit_length()) if mask >> b & 1]
    n = len(bits) // parts
    return [sum(1 << b for b in bits[k * n:(k + 1) * n]) for k in range(parts)]


def rank_program(g, core, T, topo):
    q = T.rank_of(core)
    cores = list(T.cores)
    chips = []
    for c in cores:
        if topo.chip(c) not in chips:
            chips.append(topo.chip(c))
    if topo.chip(core) not in chips:
        return
    ranks = [[r for r in range(len(cores)) if topo.chip(cores[r]) == ch] for ch in chips]
    h = chips.index(topo.chip(core))
    f = 1 - h
    near, far = ranks[h], ranks[f]
    gates = [c for c in range(64) if topo.chip(c) == chips[h] and T.rank_of(c) is None and all(topo.may_write(c, cores[d]) for d in far)]
    gates = [[c for c in gates if topo.die(c) == d][0] for d in range(2)]
    if q is None and core not in gates:
        return
    S = T.sem
    n3 = len(near) - (0 if q is None else 1)

    def did(c):
        a = topo.addr(c)
        return DstId(rid=a[0], pnc=a[1])

    A = AluOpType
    F = ActivationFunctionType
    v, s_, pe, sy = g.vector, g.scalar, g.tensor, g.sync
    cnt = {"nx": 16 * n3, "nb": 16 * n3}
    seen = {}

    def V(n, a=0, b=None, st=1, r=128):
        ar, o, w = LAY[n]
        b = w if b is None else b
        return T[ar][0:r, o + a:o + b:st] if st > 1 else T[ar][0:r, o + a:o + b]

    def inc(ins, name):
        ins.then_inc(S[name], 1)
        cnt[name] = cnt.get(name, 0) + 1

    def wt(tag, eng, *names):
        for n in names:
            key = (tag, n)
            if seen.get(key) != cnt[n]:
                eng.wait_ge(S[n], cnt[n])
                seen[key] = cnt[n]

    def wv(*n):
        wt("v", v, *n)

    def wa(*n):
        wt("a", s_, *n)

    def wp(*n):
        wt("p", pe, *n)

    def c0(s):
        return min(max(4 * (s - 1), 0), 20)

    def N(n, k):
        return "%s%d" % (n, k)

    def col(k, n=128):
        return V("cf", k, k + 1, r=n)

    mm = pe.matmul
    ts, tt = v.tensor_scalar, v.tensor_tensor
    ri, ii, fr = V("ri", 0, 1), V("ii", 0, 1), V("fr", 0, 128)

    def rows():
        wv("io")
        inc(ts(ri, V("pi", 0, 1), 4, None, A.arith_shift_right), "k_ri")
        inc(ts(ii, V("pi", 0, 1), 15, None, A.bitwise_and), "k_ri")
        inc(ts(V("frr"), fr, 4, None, A.arith_shift_right), "k_fr")
        inc(ts(V("fri"), fr, 15, None, A.bitwise_and), "k_fr")
        wv("k_ri")

    def pickers(d, so, sa, sb, sd, c):
        inc(ts(col(c), ri, float(d), None, A.is_equal), "k_cg")
        inc(ts(col(c + 1), ri, float(d), -1.0, A.is_equal, A.mult), "k_cg")
        wv("k_cg", "k_fr", "k_cf")
        inc(ts(V(so), V("fri"), col(1), col(c), A.is_equal, A.mult), "k_s")
        inc(ts(V(sa), V("fri"), col(4), col(c), A.is_equal, A.mult), "k_s")
        inc(ts(V(sb), V("fri"), col(5), col(c + 1), A.is_equal, A.mult), "k_d")
        wv("k_s")
        inc(tt(V(sd), V(so), V(sa), A.subtract), "k_d")

    def pe_base(P, D, so, sd, sb, s):
        o = s * WB + 12
        mm(P[:, 0:20], V(so), T.bx[:, o:o + 20], True, False)
        mm(D[:, 0:20], V(sd), T.bx[:, o:o + 20], True, False)
        mm(D[:, 1:20], V(sb), T.bx[:, o:o + 19], False, False)

    def pe_borders(P, D, so, sd, sb, e):
        for s in near:
            o = c0(s) - 12 * h
            b = s * WB
            w = min(12, 19 - o)
            x1 = mm(P[:, o:o + 12], V(so), T.bx[:, b:b + 12], False, s == near[-1])
            mm(D[:, o:o + 12], V(sd), T.bx[:, b:b + 12], False, False)
            x2 = mm(D[:, o + 1:o + 1 + w], V(sb), T.bx[:, b:b + w], False, s == near[-1])
        inc(x1, N("p_p", e))
        inc(x2, N("p_p", e))

    def pe_lists(p0, p, so, e):
        for j, s in enumerate(near):
            x = p[:, 32 * j:32 * j + 32] if j else p0
            mm(x, V(so), T.rx[:, s * W:s * W + 32], True, False)
            y = mm(x, V(so), T.rx[:, s * W + 32:s * W + 64], False, True)
            if j in (0, 3):
                inc(y, N("p_xl" if j else "p_x0", e))

    def places(P, D, e, out):
        def n(x):
            return V(N(x, e))
        wv(N("p_p", e), "iom")
        inc(ts(n("dk"), D[:, 0:20], 0.0, float(BIG), A.is_gt, A.mult), N("dk", e))
        wv(N("dk", e))
        inc(tt(n("sa"), P[:, 0:20], n("dk"), A.add), N("sa", e))
        wv(N("sa", e))
        inc(tt(n("sb"), n("sa"), V("trash"), A.max), N("sb", e))
        wv(N("sb", e))
        inc(ts(out, n("sb"), float(B0 - BIG), None, A.add), N("sc", e))

    inc(g.iota(V("pi", 0, 1), [[1, 1]], 0, 1), "io")
    inc(g.iota(V("fr"), [[1, 144]], 0, 0), "io")

    def trash():
        inc(g.iota(V("trash"), [[16, 20]], BIG - B0, 1, allow_small_or_imprecise_dtypes=True), "iom")

    if q is None:
        mine = far[gates.index(core)::2]
        m = topo.mask(core, cores[mine[0]])

        def send(out, src, e, sem):
            a = topo.addr(cores[mine[e]])
            g.remote_dma(out, src, sem, S.ls, a[1], a[0], m)

        trash()
        rows()
        inc(v.tensor_copy(col(1), ii), "k_cf")
        inc(ts(col(4), ii, 1.0, None, A.add), "k_cf")
        inc(ts(col(5), ii, -15.0, None, A.add), "k_cf")
        fac = (("s_o", "s_a", "s_b", "s_d"), ("ol", "oh", "m4", "hh"))
        for e in range(2):
            inc(v.memset(T.cs[:, 24 * e + 20:24 * e + 24], 0), N("xp", e))
            pickers(mine[e], *fac[e], (2, 6)[e])
        wp("k_s", "k_d", "nb")
        for e in range(2):
            so, sa, sb, sd = fac[e]
            P, D = (T.ps1, T.ps2) if e == 0 else (T.ps4, T.ps5)
            pe_base(P, D, so, sd, sb, near[0])
            pe_borders(P, D, so, sd, sb, e)
            places(P, D, e, T.cs[:, 24 * e:24 * e + 20])
            wt("g", g, N("xp", e), N("sc", e))
            send(T.fc[:], T.cs[:, 24 * e:24 * e + 24], e, S.fy)
        wp("nx")
        for e in range(2):
            X = T.ps0 if e == 0 else T.ps3
            pe_lists(X[:, 0:32], X, fac[e][0], e)
            wv(N("p_x0", e), N("p_xl", e))
            inc(v.tensor_copy(T.fs[:, 128 * e:128 * e + 128], X[:, 0:128]), N("xo", e))
            wt("g", g, N("xo", e))
            send(T.fo[:], T.fs[:, 128 * e:128 * e + 128], e, S.fx)
        for e in range(2):
            gl, gm = 256 * e, 192 * e
            v.wait_ge(S["gx%d" % e], 8 * n3)
            v.tensor_tensor(T.gm[:, gm:gm + 128], T.gl[:, gl:gl + 128], T.gl[:, gl + 128:gl + 256], A.max).then_inc(S.hm, 1)
            v.wait_ge(S.hm, e + 1)
            v.tensor_tensor(T.gm[:, gm + 128:gm + 192], T.gm[:, gm:gm + 64], T.gm[:, gm + 64:gm + 128], A.max).then_inc(S.hn, 1)
            g.wait_ge(S.hn, e + 1)
            send(T.fl[:], T.gm[:, gm + 128:gm + 192], e, S.ff)
        g.wait_ge(S.ls, 48)
        return

    me = near.index(q)
    sy.dma_start(T.endw[:], T.end[:]).then_inc(S.lde, 16)
    s_.dma_start(T.erow[:], T.end[:, c0(q):c0(q) + 12]).then_inc(S.ldr, 16)
    for k in range(8):
        (sy if k % 2 else s_).dma_start(T.v[16 * k:16 * k + 16, :], T.idx[:]).then_inc(S.ldi, 16)

    def load(k):
        sy.dma_start(T.tw[:, 4 + CUT[k]:4 + CUT[k + 1]], T.tab[:, CUT[k]:CUT[k + 1]]).then_inc(S.ldt, 16)

    load(0)
    cnt.update({"lde": 16, "ldr": 16, "ldi": 128, "ldt": 32, "fx": 8, "fy": 8, "ff": 8, "ne2": 4 * n3, "go": 1})
    inc(g.iota(V("one"), [[0, 512]], 1, 0, allow_small_or_imprecise_dtypes=True), "io1")
    inc(g.iota(V("iob"), [[1, 128]], 0, 0, allow_small_or_imprecise_dtypes=True), "k_i")
    trash()
    inc(v.memset(V("big"), 2.0 ** 99), "bg0")
    inc(v.memset(T.win[:, 0:1], 0.0), "win0")
    inc(v.memset(T.win[:, 129:130], 0.0), "win0")
    wv("bg0")
    inc(ts(V("bgc", 0, 1), V("big", 0, 1), 4.0, None, A.mult), "bg")
    inc(ts(V("bgc", 1, 2), V("big", 0, 1), -2.0, None, A.mult), "bg")
    rows()
    inc(v.tensor_copy(col(0), ri), "k_cf")
    inc(v.tensor_copy(col(1), ii), "k_cf")
    inc(ts(col(2), ri, 16.0, None, A.mult), "k_cf")
    inc(ts(col(3), ri, 16.0, 15.0, A.mult, A.add), "k_cf")
    wv("k_cf", "k_fr")
    inc(ts(V("bo"), V("frr"), col(0), None, A.is_equal), "k_b")
    wa("k_b")
    inc(s_.activation(V("nbo"), V("bo"), F.Copy, scale=-1.0), "k_n")
    inc(ts(V("rep", r=16), V("fri", r=16), col(1, 16), None, A.is_equal), "k_c")
    inc(ts(V("sel"), V("fr", 0, 16), col(1), None, A.is_equal), "k_c")
    inc(ts(V("selm"), V("fr", 0, 16), col(1), -16.0, A.is_equal, A.mult), "k_c")
    inc(ts(V("selr"), V("fr", 0, 16), col(1), col(2), A.is_equal, A.mult), "k_c")
    inc(ts(V("seln"), V("fr", 0, 16), col(1), -1.0, A.is_equal, A.mult), "k_c")
    inc(ts(V("c2"), fr, 0.0, -1536.0, A.mult, A.add), "k_c")
    inc(ts(V("zz"), V("fr"), col(3), None, A.is_equal), "k_z")
    wt("g", g, "k_n")
    inc(g.affine_select(V("nt"), V("nbo"), [[-1, 128]], A.is_ge, 0.0, 0, 1), "k_t")
    if h == 0:
        inc(g.iota(T.run0[:, B0 + 1:B0 + 1537], [[0, 1536]], 0, 0, allow_small_or_imprecise_dtypes=True), "rus0")

    def marks(k, js):
        wa("bg", "io1")
        for j in js:
            inc(s_.activation(T[N("mark", k)][:, B0 + 512 * j:B0 + 512 * j + 512], V("one"), F.Identity, bias=V("bgc", 0, 1), scale=0.0),
                N("mrk", k))

    marks(h, range(2))
    wv("ldr")
    inc(ts(V("eri", r=1), T.erow[:], 15, None, A.bitwise_and), "eri")
    wv("lde")
    inc(v.tensor_copy(V("endf", r=16), T.endw[:]), "endf")
    wv("eri")
    inc(v.tensor_copy(V("erh", r=1), V("eri", r=1)), "erh")
    wp("k_b", "k_c", "endf", "io1")
    inc(mm(T.ps5[:, 0:32], V("rep", r=16), V("endf", r=16), True, True), "p_e")
    wa("erh")
    for k in range(12):
        inc(s_.activation(V("erq", 16 * k, 16 * k + 16, r=1), V("erh", k, 192, 12, 1), F.Identity), "erq")
    wv("ldi")
    inc(ts(V("part"), T.v[:], 13, None, A.arith_shift_right), "part")
    inc(ts(V("oli", r=16), T.v[0:16, :], 127, None, A.bitwise_and), "oli")
    wv("part")
    inc(ts(V("o4"), V("part"), col(0), None, A.is_equal), "o4")
    inc(ts(V("ohi", r=16), T.v[0:16, :], 8064, None, A.bitwise_and), "oli")
    wv("o4", "io1")
    inc(v.tensor_tensor_scan(V("ic"), V("one", 0, 128), V("o4"), 0.0, A.mult, A.add), "ic")
    wp("o4", "k_t")
    mm(T.ps0[:, 0:128], V("nt"), V("o4"), True, False)
    wp("ic")
    inc(mm(T.ps0[:, 0:128], V("bo"), V("ic"), False, True), "s4")
    mm(T.ps3[:, 0:128], V("nt"), V("o4"), True, False)
    inc(mm(T.ps3[:, 0:128], V("bo"), V("ic"), False, True), "s4b")
    wv("oli")
    inc(ts(V("ol", r=16), V("oli", r=16), 4.0, None, A.add), "olh")
    inc(v.tensor_copy(V("oh", r=16), V("ohi", r=16)), "olh")
    mm(T.ps1[:, 0:16], V("c2"), V("selm"), True, False)
    mm(T.ps1[:, 0:16], V("o4"), V("selr"), False, False)
    wp("erq")
    inc(mm(T.ps6[:, 0:192], V("one", 0, 128, r=1), V("erq", r=1), True, True), "p_eb")
    wp("olh")
    mm(T.ps7[:, 0:16], V("ol", r=16), V("sel", r=16), True, True)
    mm(T.ps7[:, 16:32], V("oh", r=16), V("sel", r=16), True, True)
    mm(T.ps7[:, 32:48], V("ol", r=16), V("seln", r=16), True, True)
    inc(mm(T.ps7[:, 48:64], V("oh", r=16), V("seln", r=16), True, True), "p_ol")
    wv("s4")
    inc(tt(V("m4"), T.ps0[:, 0:128], V("o4"), A.mult), "m4")
    wv("p_e")
    inc(ts(V("eci"), T.ps5[:, c0(q):c0(q) + 12], 8.5 - 2048.0 * q, 1.0 / 16, A.add, A.mult), "eci")
    inc(ts(V("bq"), T.ps5[:, 0:32], -1023.5, 1.0 / 2048, A.add, A.mult), "bq")
    wv("m4")
    inc(ts(V("hh"), V("m4"), 1.0 / 16, 1535.53125, A.mult, A.add), "hh")
    wa("s4b", "win0")
    inc(s_.activation(T.win[:, 1:129], T.ps3[:, 0:128], F.Identity), "win")
    wp("m4")
    mm(T.ps1[:, 0:16], V("m4"), V("sel"), False, False)
    wp("hh")
    mm(T.ps1[:, 0:16], V("hh"), V("selm"), False, True)
    mm(T.ps1[:, 16:32], V("c2"), V("sel"), True, False)
    inc(mm(T.ps1[:, 16:32], V("hh"), V("sel"), False, True), "p_l3")
    wa("p_ol")
    inc(s_.activation(V("pay"), T.ps7[:, 0:64], F.Identity), "pay")
    wv("eci")
    inc(ts(V("ecl"), V("eci"), 0.0, 129.0, A.max, A.min), "ecl")
    wv("p_eb")
    inc(ts(V("mk"), T.ps6[:, 0:192], col(1), None, A.is_equal), "mk")
    wv("ecl", "win", "mk", "win0")
    inc(tt(V("yy"), T.win[:, 0:130].indirect(V("ecl")), V("mk"), A.mult), "yy")
    wv("bq")
    if h == 0:
        inc(ts(V("b0i"), V("bq", 0, 20), 0.0, 4.0, A.max, A.min), "bi")
    else:
        inc(ts(V("b0i"), V("bq", 12, 32), -4.0, 0.0, A.add, A.max), "bi")
    wv("p_l3")
    inc(v.tensor_copy(V("l3"), T.ps1[:, 0:32]), "l3")
    ev = [0, 2, 4, 6, 8, 10, 12]
    od = [i for i in range(16) if i not in ev]
    wa("l3", "pay", "k_i")
    for k, i in enumerate(od):
        inc(s_.activation(V("ta", 32 * k, 32 * k + 32), V("iob", 0, 32), F.Abs, bias=V("l3", 16 + i, 17 + i), scale=-1.0), "ta")
    wa("ta")
    for k, i in enumerate(od):
        for d in range(2):
            inc(s_.activation(T.bb[:, 64 * i + 32 * d:64 * i + 32 * d + 32], V("ta", 32 * k, 32 * k + 32), F.Relu,
                              bias=V("pay", 16 * d + i, 16 * d + i + 1), scale=V("pay", 32 + 16 * d + i, 33 + 16 * d + i)), "c%d" % i)
    marks(h, range(2, 4))
    marks(f, range(4))
    for k in range(2):
        inc(s_.activation(T[N("run", k)][:, 0:B0], V("one"), F.Identity, bias=V("bgc", 1, 2), scale=0.0), "rus")
    wp("yy", "k_z")
    for b in range(16):
        x = mm(T.ps4[:, 0:12], V("zz", 15 - b, 143 - b), V("yy", b, 192, 16), b == 0, b == 15)
    inc(x, "p_pp")
    o, ob = q * W, q * WB
    wv("l3", "pay", "k_i")
    order = ev + od
    for n, i in enumerate(order):
        inc(ts(T.aa[:, 128 * i:128 * i + 128], V("iob"), V("l3", i, i + 1), None, A.is_equal), "c%d" % i)
        if i in ev:
            for d in range(2):
                inc(ts(T.bb[:, 64 * i + 32 * d:64 * i + 32 * d + 32], V("iob", 0, 32), V("l3", 16 + i, 17 + i),
                       V("pay", 16 * d + i, 16 * d + i + 1), A.is_equal, A.mult), "c%d" % i)
        if n == 4:
            wv("p_pp", "bi")
            inc(v.tensor_copy(T.bx[:, ob:ob + 12], T.ps4[:, 0:12]), "ptx")
            inc(ts(T.bx[:, ob + 12:ob + 32], V("b0i"), 4.0, 512.0, A.min, A.mult), "ptx")
    for i in order:
        wp("c%d" % i)
        x = mm(T.ps2[:, 0:64], T.aa[:, 128 * i:128 * i + 128], T.bb[:, 64 * i:64 * i + 64], i == order[0], i == order[-1])
    inc(x, "p_x")
    wv("p_x")
    inc(v.tensor_copy(T.rx[:, o:o + 64], T.ps2[:, 0:64]), "tx")
    to = gates + [cores[r] for r in near if r != q]
    full = topo.mask(core, to[0])

    def tell(t, sem):
        g.remote_dma_fused([RemoteDMATransfer(srcs=[t], dsts=[t] * len(to), dst_ids=[did(c) for c in to], dma_engine_mask=full,
                                              remote_sem=sem)], local_sem=S.ls)

    wt("g", g, "ptx")
    tell(T.bx[:, ob:ob + WB], S.nb)
    wt("g", g, "tx")
    tell(T.rx[:, o:o + W], S.nx)
    g.sem_inc(S.go, 1)
    wt("sy", sy, "go")
    load(1)
    nls = 32
    inc(ts(col(4), ii, 1.0, None, A.add), "k_cg")
    inc(ts(col(5), ii, -15.0, None, A.add), "k_cg")
    inc(v.memset(V("src"), -2.0 ** 99), "src0")
    pickers(q, "s_o", "s_a", "s_b", "s_d", 6)
    wv("src0")
    inc(ts(V("src"), V("src"), 2.0, None, A.mult), "src")
    inc(ts(T.tw[:, 0:4], V("big"), -2.0, None, A.mult), "tws")
    for k in range(2):
        inc(ts(T[N("run", k)][:, B0:B0 + 1], V("big", 0, 1), -2.0, None, A.mult), "rus")
    inc(v.tensor_copy(V("erf", r=1), T.erow[:]), "erf")
    inc(v.memset(V("onef", r=1), 1.0), "erf")

    def XO(a, b, k):
        return T.fo[:, a:b] if k == f else V("xo0", a, b)

    def SC(a, b, k):
        return T.fc[:, a:b] if k == f else V("sc0", a, b)

    def gather(k, j, eng=s_):
        wt("v" if eng is v else "a", eng, "fx" if k == f else "xo0" if j else "xp0", "ldt", "tws")
        out = T[N("gd", k)][:, 512 * j:512 * j + 512]
        i = T.tw[:].indirect(XO(32 * j, 32 * j + 32, k))
        inc(v.tensor_copy(out, i) if eng is v else s_.activation(out, i, F.Copy), N("g" + "abcd"[j], k))

    def scatter(k):
        wv("fy" if k == f else "sc0", "src", N("mrk", k))
        inc(v.tensor_copy(T[N("mark", k)][:, 0:B0 + HB + 1].indirect(SC(0, 20, k)), V("src")), N("sct", k))

    def scan_first(j):
        run = T[N("run", h)]
        x = 512 * j
        wv(N("sct", h), "rus", N("g" + "abcd"[j], h))
        if j:
            wv("rus0")
        inc(v.tensor_tensor_scan(run[:, B0 + 1 + x:B0 + 513 + x], T[N("mark", h)][:, B0 + x:B0 + 512 + x], T[N("gd", h)][:, x:x + 512],
                                 run[:, 0:1], A.min, A.max), "rx" if j else N("ra", h))

    def scan(k, a, b):
        run = T[N("run", k)]
        x, y = 512 * a, 512 * b
        wv(N("sct", k), "rus", *[N("g" + c, k) for c in "abcd"[a:b]])
        wv(*[N("r" + c, k) for c in "abcd"[max(a - 1, 0):a]])
        inc(v.tensor_tensor_scan(run[:, B0 + 1 + x:B0 + 1 + y], T[N("mark", k)][:, B0 + x:B0 + y], T[N("gd", k)][:, x:y],
                                 run[:, B0 + x:B0 + x + 1], A.min, A.max), N("r" + "abcd"[b - 1], k))

    def pick(k, a, b, eng, sem, n=4, after=None):
        o, e = 4 * (a - 3 * k), 4 * (b + 1 - 3 * k)
        wt("v" if eng is v else "a", eng, "fy" if k == f else "sc0", "rus", after if after else N("r" + "abcd"[n - 1], k))
        out = T[N("pick", k)][:, 16 * o:16 * e]
        i = T[N("run", k)][:, 0:B0 + 512 * n + 1].indirect(SC(o, e, k))
        inc(v.tensor_copy(out, i) if eng is v else s_.activation(out, i, F.Copy), sem)

    def piece(d):
        return T.pick0[:, 64 * d:64 * (d + 1)] if d < 4 else T.pick1[:, 64 * (d - 3):64 * (d - 2)]

    def join(d, sem, *need):
        wv(*need)
        inc(tt(piece(d), T.pick0[:, 64 * d:64 * d + 64], T.pick1[:, 64 * (d - 3):64 * (d - 2)], A.max), sem)

    fb, nb = (4, 3) if h == 0 else (3, 4)
    j0 = 3 if h == 0 else 0
    rest = [j for j in range(4) if j != j0]
    P, D = T.ps3, T.ps5
    wp("k_s", "k_d", "ptx")
    pe_base(P, D, "s_o", "s_d", "s_b", q)
    wp("nb")
    pe_borders(P, D, "s_o", "s_d", "s_b", 0)
    wp("nx", "tx")
    pe_lists(T.ps2[:, 0:32], T.ps0, "s_o", 0)
    places(P, D, 0, V("sc0"))
    scatter(h)
    wv("p_x00")
    inc(v.tensor_copy(V("xo0", 0, 32), T.ps2[:, 0:32]), "xp0")
    wv("p_xl0")
    inc(v.tensor_copy(V("xo0", 32, 128), T.ps0[:, 32:128]), "xo0")
    gather(h, j0)
    gather(h, rest[0], v)
    gather(h, rest[1])
    lo = 4 * q - 1 - c0(q)
    wp("erf")
    for k in range(5):
        if lo + k >= 0:
            x = mm(T.ps7[:, 16 * k:16 * k + 16], V("onef", r=1), V("erf", lo + k, 192, 12, 1), True, True)
    inc(x, "p_z")
    scan_first(j0)
    gather(f, 0)
    pick(h, fb, fb, s_, "pfn", 4 if h == 0 else 1, "rx" if h == 0 else None)
    for j in range(1, 4):
        gather(f, j)
    scatter(f)
    scan(f, 0, 2)
    scan(f, 2, 3)
    scan(f, 3, 4)
    if h == 0:
        pick(f, fb, 5, s_, "pf", 3)
        pick(f, 6, 7, s_, "pl")
        need = (("cmf", "pf"), ("pl",))
    else:
        pick(f, 0, 1, s_, "pe", 3)
        pick(f, 2, fb, s_, "pf")
        need = (("pe",), ("pf", "cmf"))
    join(fb, "cmf", "pf", "pfn")
    ms = split(full, 2)
    for e in range(2):
        wt("g", g, *need[e])
        g.remote_dma_fused([RemoteDMATransfer(srcs=[piece(far[2 * e + k])], dsts=[T.gl[:, 256 * e + 64 * me:256 * e + 64 * me + 64]],
                                              dst_ids=[did(gates[k])], dma_engine_mask=ms[k], remote_sem=S["gx%d" % e]) for k in range(2)],
                           local_sem=S.ls)
        nls += 16
    gather(h, rest[2])
    if h == 0:
        scan(h, 0, 1)
        scan(h, 1, 2)
        pick(f, nb, nb, v, "pn")
        scan(h, 2, 4)
    else:
        scan(h, 1, 2)
        scan(h, 2, 3)
        pick(f, nb, nb, v, "pn")
        scan(h, 3, 4)
    pick(h, 2 if h == 0 else nb, nb if h == 0 else 5, v, N("pib", h))
    pick(h, near[0] if h == 0 else 6, 1 if h == 0 else near[-1], s_, N("pik", h))
    join(nb, "cmn", "pn", N("pib", h))
    ms = split(full, 4)
    wt("g", g, "cmn", N("pib", h), N("pik", h))
    g.remote_dma_fused([RemoteDMATransfer(srcs=[piece(r)], dsts=[T.nl[:, 64 * me:64 * me + 64]], dst_ids=[did(cores[r])],
                                          dma_engine_mask=ms[3 - k], remote_sem=S.ne2) for k, r in enumerate([r for r in near if r != q])],
                       local_sem=S.ls)
    nls += 4 * n3
    b0 = 0
    if lo < 0:
        inc(v.memset(V("eb", 0, 16), 0.0), "ebz")
        wv("ebz")
        b0 = 16
    wv("p_z")
    inc(v.tensor_copy(V("eb", b0, 80), T.ps7[:, b0:80]), "eb")
    wv("eb")
    inc(tt(V("ne"), V("eb", 16, 80), V("eb", 15, 79), A.is_gt), "ne")
    wv("ne")
    inc(ts(V("ze"), V("ne"), -2.0 ** 99, 0.0, A.mult, A.add), "ze")
    wv("ze")
    inc(ts(V("zf"), V("ze"), 2.0, None, A.mult), "zf")
    wv("cmn", N("pik", h), "zf")
    inc(tt(V("ya"), piece(q), V("zf"), A.max), "ya")
    nl = [T.nl[:, 64 * near.index(r):64 * near.index(r) + 64] for r in near if r != q]
    wv("ne2")
    inc(tt(V("yb"), nl[0], nl[1], A.max), "yb")
    wv("ya")
    inc(tt(V("yc"), nl[2], V("ya"), A.max), "yc")
    wv("yb", "yc")
    inc(tt(V("yd"), V("yb"), V("yc"), A.max), "yd")
    wv("yd", "ff")
    inc(tt(V("ye"), V("yd"), T.fl[:], A.max), "ye")
    wt("sy", sy, "ye")
    sy.dma_start(T.y[:], V("ye")).then_inc(S.st, 16)
    sy.wait_ge(S.st, 16)
    g.wait_ge(S.ls, nls)
